import numpy as np
import ml_dtypes


def mxq(x, axis, fmt="e4m3"):
    dtype, down = {"e4m3": (ml_dtypes.float8_e4m3fn, 7), "e5m2": (ml_dtypes.float8_e5m2, 14)}[fmt]
    v = np.moveaxis(np.asarray(x, np.float32).astype(ml_dtypes.bfloat16).astype(np.float64), axis, -1)
    blocks = v.reshape(v.shape[:-1] + (-1, 32))
    amax = np.abs(blocks).max(-1, keepdims=True)
    byte = np.maximum(np.where(amax > 0, np.frexp(amax)[1] - 1 + 127, 0) - down, 1)
    scale = np.exp2(byte - 127.0)
    codes = (blocks / scale).astype(np.float32).astype(dtype).astype(np.float64)
    return np.moveaxis((codes * scale).reshape(v.shape), -1, axis)


WIDE = False


def mx_kscale(k):
    if not WIDE:
        return np.ones(k)
    levels = np.array([10, -10, 5, -5, 0])
    if k % 512:
        return np.exp2(np.random.permutation(np.resize(levels, k // 32))).repeat(32)
    a = np.empty((k // 512, 16))
    for p in range(k // 512):
        a[p, :8] = np.random.permutation(np.resize(levels, 8))
        for g in range(8):
            far = levels[np.abs(levels - a[p, g]) >= 10]
            a[p, g + 8] = far[np.random.randint(len(far))]
    return np.exp2(a.ravel()).repeat(32)


def f64(x):
    return np.asarray(x).astype(np.float64)


def striped(idx):
    return np.tile(idx.reshape(-1, 16).T, (8, 1)).astype(np.uint16)


def unstriped(offs):
    return offs[:16].T.reshape(-1).astype(np.int64)


def gelu(v):
    return 0.5 * v * (1.0 + np.tanh(np.sqrt(2.0 / np.pi) * (v + 0.044715 * v**3)))


K, T, E, C, H, N = 1536, 1280, 4, 256, 512, 256


def by_expert(wq, xq):
    return np.concatenate([wq[e].T @ xq[:, e * C:(e + 1) * C] for e in range(E)], axis=1)


def setup_inputs():
    n = np.random.standard_normal
    s = mx_kscale(K)[:, None]
    u = mx_kscale(H)
    return {
        "xT": (n((K, T)) * s).astype(np.float32),
        "xr": n((N, T)).astype(np.float32),
        "w1": (n((E, K, H)) / np.sqrt(K) / s[None] * u[None, None, :]).astype(np.float32),
        "w2": (n((E, H, N)) / np.sqrt(H) / u[None, :, None]).astype(np.float32),
        "gate": np.tile(np.random.uniform(0.2, 1.0, E * C), (N, 1)).astype(np.float32),
        "offs": striped(np.random.permutation(T)[:E * C]),
    }


def reference(xT, xr, w1, w2, gate, offs):
    idx = unstriped(offs)
    xq = mxq(f64(xT)[:, idx], 0, "e4m3")
    h = gelu(by_expert(mxq(f64(w1), 1, "e4m3"), xq))
    y = by_expert(mxq(f64(w2), 1, "e4m3"), mxq(h, 0, "e4m3"))
    out = f64(xr).copy()
    out[:, idx] += f64(gate) * y
    return out

@@ -1,0 +1,255 @@
+from contextlib import ExitStack
+
+import concourse.mybir as mybir
+
+K, T, E, C, H, N = 1536, 1280, 4, 256, 512, 256
+S = E * C
+
+FLOPS = 2 * S * K * H + 2 * S * H * N
+BYTES = 4 * (K * T + 2 * N * T + E * K * H + E * H * N + 128 * S) + 2 * 128 * (S // 16)
+
+F32 = mybir.dt.float32
+BF16 = mybir.dt.bfloat16
+U32 = mybir.dt.uint32
+U16 = mybir.dt.uint16
+U8 = mybir.dt.uint8
+FP8X4 = mybir.dt.float8_e4m3fn_x4
+COPY = mybir.ActivationFunctionType.Copy
+GELU = mybir.ActivationFunctionType.Gelu_apprx_tanh
+MULT = mybir.AluOpType.mult
+ADD = mybir.AluOpType.add
+
+P = 128
+PASSES = K // 512
+LIST_HALF = 512
+
+X_CHUNKS = ((0, 256, "V"), (256, 512, "S"), (768, 512, "S"))
+W1_ENGINES = (("S", "S", "SV"), ("S", "SV", "S"), ("S", "SV", "S"), ("S", "SV", "SV"))
+T_ORDER = (2, 3, 0, 1)
+LIVE = {"rows": 10, "w2_rows": 3}
+LAG_QUANTIZE = 1
+LAG_GELU = 2
+LAG_HIDDEN = 3
+LAG_LEAVE = 5
+LAG_SCATTER = (6, 8)
+
+
+def tile_moe_res_mlp_gelu_kernel(tc, xT, xr, w1, w2, gate, offs, out):
+    nc = tc.nc
+    with ExitStack() as ctx:
+        keep = ctx.enter_context(tc.tile_pool(name="keep", bufs=1))
+        rows_pool = ctx.enter_context(tc.tile_pool(name="rows_pool", bufs=LIVE["rows"]))
+        w2_rows_pool = ctx.enter_context(tc.tile_pool(name="w2_rows_pool", bufs=LIVE["w2_rows"]))
+        stage = ctx.enter_context(tc.tile_pool(name="stage", bufs=4))
+        w_pool = ctx.enter_context(tc.tile_pool(name="w_pool", bufs=8))
+        w2_pool = ctx.enter_context(tc.tile_pool(name="w2_pool", bufs=3))
+        small = ctx.enter_context(tc.tile_pool(name="small", bufs=3))
+        psum1 = ctx.enter_context(tc.psum_pool(name="psum1", bufs=4))
+        psum2 = ctx.enter_context(tc.psum_pool(name="psum2", bufs=3))
+
+        offsets = keep.tile([P, S // 16], U16, name="offsets")
+        nc.sync.dma_start(offsets[:], offs)
+
+        warm = keep.tile([P, 2], F32, name="warm")
+        nc.vector.memset(warm[:], 0.0)
+        nc.scalar.activation(out=warm[:, 1:2], in_=warm[:, 0:1], func=GELU)
+
+        x_scales = keep.tile([P, T], U8, name="x_scales", align_bytes=64)
+        nc.gpsimd.memset(x_scales[:], 0)
+        sums = [keep.tile([P, T], F32, name=f"sums{b}") for b in range(2)]
+        for b in range(2):
+            nc.vector.memset(sums[b][:], 0.0)
+
+        x_codes = [keep.tile([P, T], U32, name=f"x_codes{s}", align_bytes=64) for s in range(PASSES)]
+        g_codes = [
+            [keep.tile([P, LIST_HALF], U32, name=f"g_codes{s}_{f}", align_bytes=64) for f in range(2)]
+            for s in range(PASSES)
+        ]
+        g_scales = [keep.tile([P, LIST_HALF], U8, name=f"g_scales{f}", align_bytes=64) for f in range(2)]
+        gates = keep.tile([P, S], F32, name="gates")
+        residual = [keep.tile([P, T], F32, name=f"residual{b}") for b in range(2)]
+        final = [keep.tile([P, T], F32, name=f"final{b}") for b in range(2)]
+
+        items = [("x", s, chunk) for s in range(PASSES) for chunk in range(len(X_CHUNKS))]
+        for e in range(E):
+            first = [("w1", e, s) for s in range(PASSES)]
+            second = [("w2", e, 0)]
+            items += second + first if e == 0 else first + second
+        last_item = [len(items) - (PASSES + 1) * (E - 1 - e) - 1 for e in range(E)]
+        waiting = list(reversed(items))
+        live = {"rows": 0, "w2_rows": 0}
+        loaded = {}
+
+        def ring(kind):
+            return "w2_rows" if kind == "w2" else "rows"
+
+        def load_ahead():
+            while waiting and live[ring(waiting[-1][0])] < LIVE[ring(waiting[-1][0])]:
+                item = waiting.pop()
+                kind = item[0]
+                if kind == "x":
+                    c0, width, engine = X_CHUNKS[item[2]]
+                    rows = xT[512 * item[1] : 512 * (item[1] + 1), c0 : c0 + width]
+                elif kind == "w1":
+                    rows = w1[item[1], 512 * item[2] : 512 * (item[2] + 1), :]
+                else:
+                    rows = w2[item[1]]
+                pool = w2_rows_pool if kind == "w2" else rows_pool
+                raw = pool.tile([P, 4, rows.shape[1]], F32, name=ring(kind), align_bytes=64)
+                nc.sync.dma_start(out=raw[:], in_=rows.rearrange("(p j) w -> p j w", j=4))
+                loaded[item] = raw
+                live[ring(kind)] += 1
+                if item == ("w2", 0, 0):
+                    nc.sync.dma_start(out=gates[:], in_=gate[0:P, :])
+                if not waiting:
+                    for b in range(2):
+                        nc.sync.dma_start(out=residual[b][:], in_=xr[P * b : P * (b + 1), :])
+
+        grouped = {}
+        weights = {}
+        hidden = {}
+        banks = {}
+        results = {}
+
+        def copy(engine, dst, src):
+            if engine == "V":
+                nc.vector.tensor_copy(out=dst, in_=src)
+            else:
+                nc.scalar.activation(out=dst, in_=src, func=COPY)
+
+        def interleave(item):
+            kind = item[0]
+            raw = loaded.pop(item)
+            live[ring(kind)] -= 1
+            grouped[item] = []
+            if kind == "w1":
+                engines = W1_ENGINES[item[1]][item[2]]
+                ts = 4 // len(engines)
+                src = raw[:].rearrange("p j (m t) -> p m j t", t=4)
+                for i, engine in enumerate(engines):
+                    wide = stage.tile([P, 4 * P * ts], BF16, name=f"grouped{P * ts}", align_bytes=64)
+                    dst = wide[:].rearrange("p (t m j) -> p m j t", t=ts, j=4)
+                    copy(engine, dst, src[:, :, :, ts * i : ts * (i + 1)])
+                    grouped[item].append(wide)
+            else:
+                width = raw.shape[2]
+                wide = stage.tile([P, 4 * width], BF16, name=f"grouped{width}", align_bytes=64)
+                dst = wide[:].rearrange("p (c i j) -> p c j i", i=4, j=4)
+                src = raw[:].rearrange("p j (c i) -> p c j i", i=4)
+                copy(X_CHUNKS[item[2]][2] if kind == "x" else "V", dst, src)
+                grouped[item].append(wide)
+
+        def quantize(item):
+            kind, e, s = item
+            if kind == "x":
+                c0, width, engine = X_CHUNKS[s]
+                codes, scales = x_codes[e][:, c0 : c0 + width], x_scales[4 * e : P, c0 : c0 + width]
+            elif kind == "w1":
+                w1_codes = w_pool.tile([P, H], U32, name="w1_codes", align_bytes=64)
+                w1_scales = w_pool.tile([P, H], U8, name="w1_scales", align_bytes=64)
+                weights[item] = (w1_codes, w1_scales)
+                codes, scales = w1_codes[:], w1_scales[:]
+            else:
+                w2_codes = w2_pool.tile([P, N], U32, name="w2_codes", align_bytes=64)
+                w2_scales = w2_pool.tile([P, N], U8, name="w2_scales", align_bytes=64)
+                weights[item] = (w2_codes, w2_scales)
+                codes, scales = w2_codes[:], w2_scales[:]
+            pieces = grouped.pop(item)
+            width = codes.shape[1] // len(pieces)
+            for i in reversed(range(len(pieces))):
+                cols = slice(width * i, width * (i + 1))
+                nc.vector.quantize_mx(out=codes[:, cols].bitcast(FP8X4), scales=scales[:, cols], in_=pieces[i][:])
+
+        def gather(target, window, f):
+            nc.vector.tensor_copy(target[f][:], window[:].indirect(offsets[:, 32 * f : 32 * (f + 1)]))
+
+        def first_layer(e, part):
+            f, at = divmod(C * e + P * part, LIST_HALF)
+            a_bank = psum1.tile([P, 4, P], F32, name="a_bank")
+            for t in T_ORDER:
+                rows = slice(P * t, P * (t + 1))
+                for s in range(PASSES):
+                    codes, scales = weights["w1", e, s]
+                    nc.tensor.matmul_mx(
+                        out=a_bank[:, t, :],
+                        lhsT=codes[:, rows].bitcast(FP8X4),
+                        lhsT_scale=scales[:, rows],
+                        rhs=g_codes[s][f][:, at : at + P].bitcast(FP8X4),
+                        rhs_scale=g_scales[f][4 * s : P, at : at + P],
+                        start=(s == 0),
+                        stop=(s == PASSES - 1),
+                    )
+            h = small.tile([P, 4 * P], BF16, name="h", align_bytes=64)
+            nc.scalar.activation(
+                out=h[:].rearrange("p (n t) -> p n t", t=4), in_=a_bank[:].rearrange("p t n -> p n t"), func=GELU
+            )
+            hidden[e, part] = h
+
+        def second_layer(e):
+            h_codes = small.tile([P, C], U32, name="h_codes", align_bytes=64)
+            h_scales = small.tile([P, C], U8, name="h_scales", align_bytes=64)
+            for part in range(2):
+                cols = slice(P * part, P * (part + 1))
+                nc.vector.quantize_mx(
+                    out=h_codes[:, cols].bitcast(FP8X4), scales=h_scales[:, cols], in_=hidden[e, part][:]
+                )
+            codes, scales = weights["w2", e, 0]
+            y_bank = psum2.tile([P, 2, C], F32, name="y_bank")
+            for b in range(2):
+                rows = slice(P * b, P * (b + 1))
+                nc.tensor.matmul_mx(
+                    out=y_bank[:, b, :],
+                    lhsT=codes[:, rows].bitcast(FP8X4),
+                    lhsT_scale=scales[:, rows],
+                    rhs=h_codes[:].bitcast(FP8X4),
+                    rhs_scale=h_scales[:],
+                    start=True,
+                    stop=True,
+                )
+            banks[e] = y_bank
+
+        def leave_bank(e):
+            y = small.tile([P, 2, C], F32, name="y")
+            for b in range(2):
+                nc.scalar.copy(out=y[:, b, :], in_=banks[e][:, b, :])
+            results[e] = y
+
+        def put_back(e, b):
+            nc.vector.tensor_tensor(
+                sums[b][:].indirect(offsets[:, 16 * e : 16 * (e + 1)]),
+                results[e][:, b, :],
+                gates[:, C * e : C * (e + 1)],
+                MULT,
+            )
+
+        load_ahead()
+        for step in range(len(items) + LAG_SCATTER[1]):
+            if step < len(items):
+                interleave(items[step])
+                load_ahead()
+            if LAG_QUANTIZE <= step < len(items) + LAG_QUANTIZE:
+                item = items[step - LAG_QUANTIZE]
+                quantize(item)
+                if item[0] == "x" and item[2] == len(X_CHUNKS) - 1:
+                    for f in range(2):
+                        gather(g_codes[item[1]], x_codes[item[1]], f)
+                        if item[1] == PASSES - 1:
+                            gather(g_scales, x_scales, f)
+            for e in range(E):
+                if step - last_item[e] == LAG_GELU:
+                    first_layer(e, 0)
+                    first_layer(e, 1)
+            for e in range(E):
+                lag = step - last_item[e]
+                if lag == LAG_HIDDEN:
+                    second_layer(e)
+                if lag == LAG_LEAVE:
+                    leave_bank(e)
+                for b in range(2):
+                    if lag == LAG_SCATTER[b]:
+                        put_back(e, b)
+        for b in range(2):
+            for q in range(2):
+                cols = slice(640 * q, 640 * (q + 1))
+                nc.vector.tensor_tensor(final[b][:, cols], sums[b][:, cols], residual[b][:, cols], ADD)
+                nc.sync.dma_start(out=out[P * b : P * (b + 1), cols], in_=final[b][:, cols])

@@ -22,40 +22,30 @@ ADD = mybir.AluOpType.add
 P = 128
 PASSES = K // 512
 LIST_HALF = 512
-
 X_CHUNKS = ((0, 256, "V"), (256, 512, "S"), (768, 512, "S"))
-W1_ENGINES = (("S", "S", "SV"), ("S", "SV", "S"), ("S", "SV", "S"), ("S", "SV", "SV"))
-T_ORDER = (2, 3, 0, 1)
-LIVE = {"rows": 10, "w2_rows": 3}
-LAG_QUANTIZE = 1
-LAG_GELU = 2
-LAG_HIDDEN = 3
-LAG_LEAVE = 5
-LAG_SCATTER = (6, 8)
+RING = 14
 
 
 def tile_moe_res_mlp_gelu_kernel(tc, xT, xr, w1, w2, gate, offs, out):
     nc = tc.nc
     with ExitStack() as ctx:
         keep = ctx.enter_context(tc.tile_pool(name="keep", bufs=1))
-        rows_pool = ctx.enter_context(tc.tile_pool(name="rows_pool", bufs=LIVE["rows"]))
-        w2_rows_pool = ctx.enter_context(tc.tile_pool(name="w2_rows_pool", bufs=LIVE["w2_rows"]))
+        rows_pool = ctx.enter_context(tc.tile_pool(name="rows_pool", bufs=RING))
         stage = ctx.enter_context(tc.tile_pool(name="stage", bufs=4))
-        w_pool = ctx.enter_context(tc.tile_pool(name="w_pool", bufs=8))
-        w2_pool = ctx.enter_context(tc.tile_pool(name="w2_pool", bufs=3))
+        pair_stage = ctx.enter_context(tc.tile_pool(name="pair_stage", bufs=2))
+        w_pool = ctx.enter_context(tc.tile_pool(name="w_pool", bufs=2))
         small = ctx.enter_context(tc.tile_pool(name="small", bufs=3))
         psum1 = ctx.enter_context(tc.psum_pool(name="psum1", bufs=4))
         psum2 = ctx.enter_context(tc.psum_pool(name="psum2", bufs=3))
 
         offsets = keep.tile([P, S // 16], U16, name="offsets")
-        nc.sync.dma_start(offsets[:], offs)
 
         warm = keep.tile([P, 2], F32, name="warm")
         nc.vector.memset(warm[:], 0.0)
         nc.scalar.activation(out=warm[:, 1:2], in_=warm[:, 0:1], func=GELU)
 
         x_scales = keep.tile([P, T], U8, name="x_scales", align_bytes=64)
-        nc.gpsimd.memset(x_scales[:], 0)
+        nc.vector.memset(x_scales[:].bitcast(U32), 0)
         sums = [keep.tile([P, T], F32, name=f"sums{b}") for b in range(2)]
         for b in range(2):
             nc.vector.memset(sums[b][:], 0.0)
@@ -66,44 +56,44 @@ def tile_moe_res_mlp_gelu_kernel(tc, xT, xr, w1, w2, gate, offs, out):
             for s in range(PASSES)
         ]
         g_scales = [keep.tile([P, LIST_HALF], U8, name=f"g_scales{f}", align_bytes=64) for f in range(2)]
-        gates = keep.tile([P, S], F32, name="gates")
-        residual = [keep.tile([P, T], F32, name=f"residual{b}") for b in range(2)]
-        final = [keep.tile([P, T], F32, name=f"final{b}") for b in range(2)]
+        gates = {}
+        residual = {}
+        w2_rows = {}
+        w2_codes = [keep.tile([P, N], U32, name=f"w2_codes{e}", align_bytes=64) for e in range(E)]
+        w2_scales = [keep.tile([P, N], U8, name=f"w2_scales{e}", align_bytes=64) for e in range(E)]
 
         items = [("x", s, chunk) for s in range(PASSES) for chunk in range(len(X_CHUNKS))]
         for e in range(E):
-            first = [("w1", e, s) for s in range(PASSES)]
-            second = [("w2", e, 0)]
-            items += second + first if e == 0 else first + second
-        last_item = [len(items) - (PASSES + 1) * (E - 1 - e) - 1 for e in range(E)]
-        waiting = list(reversed(items))
-        live = {"rows": 0, "w2_rows": 0}
+            items += [("w1", e, s) for s in range(PASSES)] + [("w2", e, 0)]
+        last_w1 = [items.index(("w1", e, PASSES - 1)) for e in range(E)]
         loaded = {}
 
-        def ring(kind):
-            return "w2_rows" if kind == "w2" else "rows"
-
-        def load_ahead():
-            while waiting and live[ring(waiting[-1][0])] < LIVE[ring(waiting[-1][0])]:
-                item = waiting.pop()
-                kind = item[0]
-                if kind == "x":
-                    c0, width, engine = X_CHUNKS[item[2]]
-                    rows = xT[512 * item[1] : 512 * (item[1] + 1), c0 : c0 + width]
-                elif kind == "w1":
-                    rows = w1[item[1], 512 * item[2] : 512 * (item[2] + 1), :]
-                else:
-                    rows = w2[item[1]]
-                pool = w2_rows_pool if kind == "w2" else rows_pool
-                raw = pool.tile([P, 4, rows.shape[1]], F32, name=ring(kind), align_bytes=64)
-                nc.sync.dma_start(out=raw[:], in_=rows.rearrange("(p j) w -> p j w", j=4))
-                loaded[item] = raw
-                live[ring(kind)] += 1
-                if item == ("w2", 0, 0):
-                    nc.sync.dma_start(out=gates[:], in_=gate[0:P, :])
-                if not waiting:
-                    for b in range(2):
-                        nc.sync.dma_start(out=residual[b][:], in_=xr[P * b : P * (b + 1), :])
+        def load(item):
+            kind, a, b = item
+            if kind == "w2":
+                w2_rows[a] = rows_pool.tile([P, 4, N], F32, name="rows", align_bytes=64)
+                rows = w2[a].rearrange("(q t u) n -> u q t n", t=4, u=2)
+                for u in range(2):
+                    nc.sync.dma_start(out=w2_rows[a][u:P:2], in_=rows[u])
+                if a % 2 == 0:
+                    f = a // 2
+                    gates[f] = rows_pool.tile([P, LIST_HALF], F32, name="rows", align_bytes=64)
+                    nc.sync.dma_start(out=gates[f][:], in_=gate[0:P, LIST_HALF * f : LIST_HALF * (f + 1)])
+                if a == E - 1:
+                    for c in range(2):
+                        residual[c] = rows_pool.tile([P, T], F32, name="rows", align_bytes=64)
+                        nc.sync.dma_start(out=residual[c][:], in_=xr[P * c : P * (c + 1), :])
+                return
+            if kind == "x":
+                c0, width, engine = X_CHUNKS[b]
+                rows = xT[512 * a : 512 * (a + 1), c0 : c0 + width]
+            else:
+                rows = w1[a, 512 * b : 512 * (b + 1), :]
+            raw = rows_pool.tile([P, 4, rows.shape[1]], F32, name="rows", align_bytes=64)
+            nc.sync.dma_start(out=raw[:], in_=rows.rearrange("(p j) w -> p j w", j=4))
+            loaded[item] = raw
+            if item == ("x", 0, 1):
+                nc.sync.dma_start(offsets[:], offs)
 
         grouped = {}
         weights = {}
@@ -111,54 +101,64 @@ def tile_moe_res_mlp_gelu_kernel(tc, xT, xr, w1, w2, gate, offs, out):
         banks = {}
         results = {}
 
-        def copy(engine, dst, src):
+        def side_by_side(engine, dst, src):
+            dst = dst.rearrange("p (c i j) -> p c j i", i=2, j=4)
+            src = src.rearrange("p j (c i) -> p c j i", i=2)
             if engine == "V":
                 nc.vector.tensor_copy(out=dst, in_=src)
             else:
                 nc.scalar.activation(out=dst, in_=src, func=COPY)
 
         def interleave(item):
-            kind = item[0]
-            raw = loaded.pop(item)
-            live[ring(kind)] -= 1
-            grouped[item] = []
+            kind, a, b = item
             if kind == "w1":
-                engines = W1_ENGINES[item[1]][item[2]]
-                ts = 4 // len(engines)
-                src = raw[:].rearrange("p j (m t) -> p m j t", t=4)
-                for i, engine in enumerate(engines):
-                    wide = stage.tile([P, 4 * P * ts], BF16, name=f"grouped{P * ts}", align_bytes=64)
-                    dst = wide[:].rearrange("p (t m j) -> p m j t", t=ts, j=4)
-                    copy(engine, dst, src[:, :, :, ts * i : ts * (i + 1)])
-                    grouped[item].append(wide)
+                src = loaded[item][:].rearrange("p j (q t u) -> p t q j u", t=4, u=2)
+                if b == 0:
+                    grouped[item] = stage.tile([P, 4 * H], BF16, name="wide", align_bytes=64)
+                    wide = grouped[item][:]
+                elif b == 1:
+                    grouped[item] = pair_stage.tile([P, 8 * H], BF16, name="pair", align_bytes=64)
+                    wide = grouped[item][:, 0 : 4 * H]
+                else:
+                    wide = grouped["w1", a, 1][:, 4 * H : 8 * H]
+                dst = wide.rearrange("p (t q u j) -> p t q j u", t=4, u=2, j=4)
+                if b == PASSES - 1 and a > 0:
+                    nc.vector.tensor_copy(out=dst, in_=src)
+                else:
+                    nc.scalar.copy(out=dst, in_=src)
+            elif kind == "x":
+                raw = loaded.pop(item)
+                c0, width, engine = X_CHUNKS[b]
+                wide = stage.tile([P, 4 * width], BF16, name="wide", align_bytes=64)
+                side_by_side(engine, wide[:], raw[:])
+                grouped[item] = wide
             else:
-                width = raw.shape[2]
-                wide = stage.tile([P, 4 * width], BF16, name=f"grouped{width}", align_bytes=64)
-                dst = wide[:].rearrange("p (c i j) -> p c j i", i=4, j=4)
-                src = raw[:].rearrange("p j (c i) -> p c j i", i=4)
-                copy(X_CHUNKS[item[2]][2] if kind == "x" else "V", dst, src)
-                grouped[item].append(wide)
+                wide = stage.tile([P, 4 * N], BF16, name="wide", align_bytes=64)
+                side_by_side("S", wide[:], w2_rows[a][:])
+                grouped[item] = wide
 
         def quantize(item):
-            kind, e, s = item
+            kind, a, b = item
             if kind == "x":
-                c0, width, engine = X_CHUNKS[s]
-                codes, scales = x_codes[e][:, c0 : c0 + width], x_scales[4 * e : P, c0 : c0 + width]
+                c0, width, engine = X_CHUNKS[b]
+                cols = slice(c0, c0 + width)
+                nc.vector.quantize_mx(
+                    out=x_codes[a][:, cols].bitcast(FP8X4), scales=x_scales[4 * a : P, cols], in_=grouped.pop(item)[:]
+                )
             elif kind == "w1":
-                w1_codes = w_pool.tile([P, H], U32, name="w1_codes", align_bytes=64)
-                w1_scales = w_pool.tile([P, H], U8, name="w1_scales", align_bytes=64)
-                weights[item] = (w1_codes, w1_scales)
-                codes, scales = w1_codes[:], w1_scales[:]
+                if b == 0:
+                    codes = w_pool.tile([P, PASSES * H], U32, name="w1_codes", align_bytes=64)
+                    scales = w_pool.tile([P, PASSES * H], U8, name="w1_scales", align_bytes=64)
+                    weights[a] = (codes, scales)
+                codes, scales = weights[a]
+                if b != 1:
+                    cols = slice(0, H) if b == 0 else slice(H, PASSES * H)
+                    wide = grouped.pop(("w1", a, min(b, 1)))
+                    nc.vector.quantize_mx(out=codes[:, cols].bitcast(FP8X4), scales=scales[:, cols], in_=wide[:])
             else:
-                w2_codes = w2_pool.tile([P, N], U32, name="w2_codes", align_bytes=64)
-                w2_scales = w2_pool.tile([P, N], U8, name="w2_scales", align_bytes=64)
-                weights[item] = (w2_codes, w2_scales)
-                codes, scales = w2_codes[:], w2_scales[:]
-            pieces = grouped.pop(item)
-            width = codes.shape[1] // len(pieces)
-            for i in reversed(range(len(pieces))):
-                cols = slice(width * i, width * (i + 1))
-                nc.vector.quantize_mx(out=codes[:, cols].bitcast(FP8X4), scales=scales[:, cols], in_=pieces[i][:])
+                nc.vector.quantize_mx(
+                    out=w2_codes[a][:].bitcast(FP8X4), scales=w2_scales[a][:], in_=grouped.pop(item)[:]
+                )
 
         def gather(target, window, f):
             nc.vector.tensor_copy(target[f][:], window[:].indirect(offsets[:, 32 * f : 32 * (f + 1)]))
@@ -166,10 +166,10 @@ def tile_moe_res_mlp_gelu_kernel(tc, xT, xr, w1, w2, gate, offs, out):
         def first_layer(e, part):
             f, at = divmod(C * e + P * part, LIST_HALF)
             a_bank = psum1.tile([P, 4, P], F32, name="a_bank")
-            for t in T_ORDER:
-                rows = slice(P * t, P * (t + 1))
+            for t in range(4):
                 for s in range(PASSES):
-                    codes, scales = weights["w1", e, s]
+                    rows = slice(H * s + P * t, H * s + P * (t + 1))
+                    codes, scales = weights[e]
                     nc.tensor.matmul_mx(
                         out=a_bank[:, t, :],
                         lhsT=codes[:, rows].bitcast(FP8X4),
@@ -179,28 +179,26 @@ def tile_moe_res_mlp_gelu_kernel(tc, xT, xr, w1, w2, gate, offs, out):
                         start=(s == 0),
                         stop=(s == PASSES - 1),
                     )
-            h = small.tile([P, 4 * P], BF16, name="h", align_bytes=64)
+            if part == 0 and e < E - 1:
+                hidden[e] = loaded["w1", e + 1, 0][:, 0, :].bitcast(BF16)
+            elif part == 0:
+                hidden[e] = small.tile([P, 4 * C], BF16, name="h", align_bytes=64)[:]
+            h = hidden[e][:, 4 * P * part : 4 * P * (part + 1)]
             nc.scalar.activation(
-                out=h[:].rearrange("p (n t) -> p n t", t=4), in_=a_bank[:].rearrange("p t n -> p n t"), func=GELU
+                out=h.rearrange("p (n t) -> p n t", t=4), in_=a_bank[:].rearrange("p t n -> p n t"), func=GELU
             )
-            hidden[e, part] = h
 
         def second_layer(e):
             h_codes = small.tile([P, C], U32, name="h_codes", align_bytes=64)
             h_scales = small.tile([P, C], U8, name="h_scales", align_bytes=64)
-            for part in range(2):
-                cols = slice(P * part, P * (part + 1))
-                nc.vector.quantize_mx(
-                    out=h_codes[:, cols].bitcast(FP8X4), scales=h_scales[:, cols], in_=hidden[e, part][:]
-                )
-            codes, scales = weights["w2", e, 0]
+            nc.vector.quantize_mx(out=h_codes[:].bitcast(FP8X4), scales=h_scales[:], in_=hidden[e])
             y_bank = psum2.tile([P, 2, C], F32, name="y_bank")
             for b in range(2):
                 rows = slice(P * b, P * (b + 1))
                 nc.tensor.matmul_mx(
                     out=y_bank[:, b, :],
-                    lhsT=codes[:, rows].bitcast(FP8X4),
-                    lhsT_scale=scales[:, rows],
+                    lhsT=w2_codes[e][:, rows].bitcast(FP8X4),
+                    lhsT_scale=w2_scales[e][:, rows],
                     rhs=h_codes[:].bitcast(FP8X4),
                     rhs_scale=h_scales[:],
                     start=True,
@@ -209,47 +207,62 @@ def tile_moe_res_mlp_gelu_kernel(tc, xT, xr, w1, w2, gate, offs, out):
             banks[e] = y_bank
 
         def leave_bank(e):
-            y = small.tile([P, 2, C], F32, name="y")
-            for b in range(2):
-                nc.scalar.copy(out=y[:, b, :], in_=banks[e][:, b, :])
+            if e < E - 2:
+                y = w2_rows[e + 1][:, 0:2, :]
+            elif e == E - 2:
+                y = loaded["w1", e + 1, 1][:, 0, :].rearrange("p (b n) -> p b n", b=2)
+            else:
+                y = small.tile([P, 2, C], F32, name="y")[:]
+            if e < E - 1:
+                nc.scalar.copy(out=y, in_=banks[e][:])
+            else:
+                for b in range(2):
+                    nc.scalar.copy(out=y[:, b, :], in_=banks[e][:, b, :])
             results[e] = y
 
         def put_back(e, b):
+            f, at = divmod(C * e, LIST_HALF)
             nc.vector.tensor_tensor(
                 sums[b][:].indirect(offsets[:, 16 * e : 16 * (e + 1)]),
                 results[e][:, b, :],
-                gates[:, C * e : C * (e + 1)],
+                gates[f][:, at : at + C],
                 MULT,
             )
 
-        load_ahead()
-        for step in range(len(items) + LAG_SCATTER[1]):
-            if step < len(items):
-                interleave(items[step])
-                load_ahead()
-            if LAG_QUANTIZE <= step < len(items) + LAG_QUANTIZE:
-                item = items[step - LAG_QUANTIZE]
-                quantize(item)
-                if item[0] == "x" and item[2] == len(X_CHUNKS) - 1:
-                    for f in range(2):
-                        gather(g_codes[item[1]], x_codes[item[1]], f)
-                        if item[1] == PASSES - 1:
-                            gather(g_scales, x_scales, f)
-            for e in range(E):
-                if step - last_item[e] == LAG_GELU:
-                    first_layer(e, 0)
-                    first_layer(e, 1)
-            for e in range(E):
-                lag = step - last_item[e]
-                if lag == LAG_HIDDEN:
-                    second_layer(e)
-                if lag == LAG_LEAVE:
-                    leave_bank(e)
-                for b in range(2):
-                    if lag == LAG_SCATTER[b]:
-                        put_back(e, b)
-        for b in range(2):
+        def finish(b):
             for q in range(2):
                 cols = slice(640 * q, 640 * (q + 1))
-                nc.vector.tensor_tensor(final[b][:, cols], sums[b][:, cols], residual[b][:, cols], ADD)
-                nc.sync.dma_start(out=out[P * b : P * (b + 1), cols], in_=final[b][:, cols])
+                nc.vector.tensor_tensor(residual[b][:, cols], sums[b][:, cols], residual[b][:, cols], ADD)
+                nc.sync.dma_start(out=out[P * b : P * (b + 1), cols], in_=residual[b][:, cols])
+
+        ahead = RING - 5
+        for item in items[:ahead]:
+            load(item)
+        for step in range(len(items) + 7):
+            if step < len(items):
+                interleave(items[step])
+            if step + ahead < len(items):
+                load(items[step + ahead])
+            if 1 <= step <= len(items):
+                item = items[step - 1]
+                quantize(item)
+                if item[0] == "x" and item[2] == len(X_CHUNKS) - 1:
+                    s = item[1]
+                    for f in range(2):
+                        gather(g_codes[s], x_codes[s], f)
+                        if s == PASSES - 1:
+                            gather(g_scales, x_scales, f)
+            for e in range(E):
+                lag = step - last_w1[e]
+                if lag == 2:
+                    first_layer(e, 0)
+                    first_layer(e, 1)
+                if lag == 3:
+                    second_layer(e)
+                if lag == 5:
+                    leave_bank(e)
+                if lag == 6:
+                    for b in range(2):
+                        put_back(e, b)
+                        if e == E - 1:
+                            finish(b)

@@ -22,15 +22,18 @@ ADD = mybir.AluOpType.add
 P = 128
 PASSES = K // 512
 LIST_HALF = 512
-X_CHUNKS = ((0, 256, "V"), (256, 512, "S"), (768, 512, "S"))
-RING = 14
+X_CHUNKS = ((0, 512), (512, 512), (1024, 256))
+SLOT = 4 * H * 4
+SLOTS = 15
+X_BYTES = 4 * T * 4
+FIRST_FREE = 8
 
 
 def tile_moe_res_mlp_gelu_kernel(tc, xT, xr, w1, w2, gate, offs, out):
     nc = tc.nc
     with ExitStack() as ctx:
         keep = ctx.enter_context(tc.tile_pool(name="keep", bufs=1))
-        rows_pool = ctx.enter_context(tc.tile_pool(name="rows_pool", bufs=RING))
+        rows_pool = ctx.enter_context(tc.tile_pool(name="rows_pool", bufs=1))
         stage = ctx.enter_context(tc.tile_pool(name="stage", bufs=4))
         pair_stage = ctx.enter_context(tc.tile_pool(name="pair_stage", bufs=2))
         w_pool = ctx.enter_context(tc.tile_pool(name="w_pool", bufs=2))
@@ -67,33 +70,44 @@ def tile_moe_res_mlp_gelu_kernel(tc, xT, xr, w1, w2, gate, offs, out):
             items += [("w1", e, s) for s in range(PASSES)] + [("w2", e, 0)]
         last_w1 = [items.index(("w1", e, PASSES - 1)) for e in range(E)]
         loaded = {}
+        slots = []
+
+        def slot(shape):
+            number = len(slots)
+            slots.append(
+                rows_pool.tile(
+                    shape, F32, name=f"rows{number}", align_bytes=64, offset=SLOT * ((FIRST_FREE + number) % SLOTS)
+                )
+            )
+            return slots[-1]
+
+        def load_gates(f):
+            gates[f] = slot([P, LIST_HALF])
+            nc.sync.dma_start(out=gates[f][:], in_=gate[0:P, LIST_HALF * f : LIST_HALF * (f + 1)])
 
         def load(item):
             kind, a, b = item
-            if kind == "w2":
-                w2_rows[a] = rows_pool.tile([P, 4, N], F32, name="rows", align_bytes=64)
-                rows = w2[a].rearrange("(q t u) n -> u q t n", t=4, u=2)
-                for u in range(2):
-                    nc.sync.dma_start(out=w2_rows[a][u:P:2], in_=rows[u])
-                if a % 2 == 0:
-                    f = a // 2
-                    gates[f] = rows_pool.tile([P, LIST_HALF], F32, name="rows", align_bytes=64)
-                    nc.sync.dma_start(out=gates[f][:], in_=gate[0:P, LIST_HALF * f : LIST_HALF * (f + 1)])
-                if a == E - 1:
-                    for c in range(2):
-                        residual[c] = rows_pool.tile([P, T], F32, name="rows", align_bytes=64)
-                        nc.sync.dma_start(out=residual[c][:], in_=xr[P * c : P * (c + 1), :])
-                return
             if kind == "x":
-                c0, width, engine = X_CHUNKS[b]
-                rows = xT[512 * a : 512 * (a + 1), c0 : c0 + width]
-            else:
+                if b == 0:
+                    loaded[a] = rows_pool.tile([P, 4, T], F32, name=f"x_rows{a}", align_bytes=64, offset=X_BYTES * a)
+                    rows = xT[512 * a : 512 * (a + 1), :]
+                    nc.sync.dma_start(out=loaded[a][:], in_=rows.rearrange("(p j) w -> p j w", j=4))
+                if item == ("x", 1, 0):
+                    nc.sync.dma_start(offsets[:], offs)
+            elif kind == "w1":
+                loaded[item] = slot([P, 4, H])
                 rows = w1[a, 512 * b : 512 * (b + 1), :]
-            raw = rows_pool.tile([P, 4, rows.shape[1]], F32, name="rows", align_bytes=64)
-            nc.sync.dma_start(out=raw[:], in_=rows.rearrange("(p j) w -> p j w", j=4))
-            loaded[item] = raw
-            if item == ("x", 0, 1):
-                nc.sync.dma_start(offsets[:], offs)
+                nc.sync.dma_start(out=loaded[item][:], in_=rows.rearrange("(p j) w -> p j w", j=4))
+            else:
+                if a == 1:
+                    load_gates(0)
+                w2_rows[a] = slot([P, 4, N])
+                nc.sync.dma_start(out=w2_rows[a][:], in_=w2[a].rearrange("(p j) w -> p j w", j=4))
+                if a == E - 1:
+                    load_gates(1)
+                    for c in range(2):
+                        residual[c] = slot([P, T])
+                        nc.sync.dma_start(out=residual[c][:], in_=xr[P * c : P * (c + 1), :])
 
         grouped = {}
         weights = {}
@@ -102,8 +116,8 @@ def tile_moe_res_mlp_gelu_kernel(tc, xT, xr, w1, w2, gate, offs, out):
         results = {}
 
         def side_by_side(engine, dst, src):
-            dst = dst.rearrange("p (c i j) -> p c j i", i=2, j=4)
-            src = src.rearrange("p j (c i) -> p c j i", i=2)
+            dst = dst.rearrange("p (c i j) -> p c j i", i=4, j=4)
+            src = src.rearrange("p j (c i) -> p c j i", i=4)
             if engine == "V":
                 nc.vector.tensor_copy(out=dst, in_=src)
             else:
@@ -112,7 +126,7 @@ def tile_moe_res_mlp_gelu_kernel(tc, xT, xr, w1, w2, gate, offs, out):
         def interleave(item):
             kind, a, b = item
             if kind == "w1":
-                src = loaded[item][:].rearrange("p j (q t u) -> p t q j u", t=4, u=2)
+                src = loaded[item][:].rearrange("p j (m t) -> p m j t", t=4)
                 if b == 0:
                     grouped[item] = stage.tile([P, 4 * H], BF16, name="wide", align_bytes=64)
                     wide = grouped[item][:]
@@ -121,16 +135,16 @@ def tile_moe_res_mlp_gelu_kernel(tc, xT, xr, w1, w2, gate, offs, out):
                     wide = grouped[item][:, 0 : 4 * H]
                 else:
                     wide = grouped["w1", a, 1][:, 4 * H : 8 * H]
-                dst = wide.rearrange("p (t q u j) -> p t q j u", t=4, u=2, j=4)
+                dst = wide.rearrange("p (t m j) -> p m j t", t=4, j=4)
                 if b == PASSES - 1 and a > 0:
                     nc.vector.tensor_copy(out=dst, in_=src)
                 else:
                     nc.scalar.copy(out=dst, in_=src)
             elif kind == "x":
-                raw = loaded.pop(item)
-                c0, width, engine = X_CHUNKS[b]
+                c0, width = X_CHUNKS[b]
+                engine = "V" if b == 1 or (b == 2 and a == PASSES - 1) else "S"
                 wide = stage.tile([P, 4 * width], BF16, name="wide", align_bytes=64)
-                side_by_side(engine, wide[:], raw[:])
+                side_by_side(engine, wide[:], loaded[a][:, :, c0 : c0 + width])
                 grouped[item] = wide
             else:
                 wide = stage.tile([P, 4 * N], BF16, name="wide", align_bytes=64)
@@ -140,7 +154,7 @@ def tile_moe_res_mlp_gelu_kernel(tc, xT, xr, w1, w2, gate, offs, out):
         def quantize(item):
             kind, a, b = item
             if kind == "x":
-                c0, width, engine = X_CHUNKS[b]
+                c0, width = X_CHUNKS[b]
                 cols = slice(c0, c0 + width)
                 nc.vector.quantize_mx(
                     out=x_codes[a][:, cols].bitcast(FP8X4), scales=x_scales[4 * a : P, cols], in_=grouped.pop(item)[:]
@@ -230,12 +244,12 @@ def tile_moe_res_mlp_gelu_kernel(tc, xT, xr, w1, w2, gate, offs, out):
             )
 
         def finish(b):
-            for q in range(2):
-                cols = slice(640 * q, 640 * (q + 1))
+            for c0, c1 in ((0, T),) if b == 0 else ((0, 896), (896, T)):
+                cols = slice(c0, c1)
                 nc.vector.tensor_tensor(residual[b][:, cols], sums[b][:, cols], residual[b][:, cols], ADD)
                 nc.sync.dma_start(out=out[P * b : P * (b + 1), cols], in_=residual[b][:, cols])
 
-        ahead = RING - 5
+        ahead = 12
         for item in items[:ahead]:
             load(item)
         for step in range(len(items) + 7):

@@ -35,7 +35,8 @@ def tile_moe_res_mlp_gelu_kernel(tc, xT, xr, w1, w2, gate, offs, out):
         keep = ctx.enter_context(tc.tile_pool(name="keep", bufs=1))
         rows_pool = ctx.enter_context(tc.tile_pool(name="rows_pool", bufs=1))
         stage = ctx.enter_context(tc.tile_pool(name="stage", bufs=4))
-        pair_stage = ctx.enter_context(tc.tile_pool(name="pair_stage", bufs=2))
+        shared = ctx.enter_context(tc.tile_pool(name="shared", bufs=1))
+        pair_stage = ctx.enter_context(tc.tile_pool(name="pair_stage", bufs=1))
         w_pool = ctx.enter_context(tc.tile_pool(name="w_pool", bufs=2))
         small = ctx.enter_context(tc.tile_pool(name="small", bufs=3))
         psum1 = ctx.enter_context(tc.psum_pool(name="psum1", bufs=4))
@@ -54,11 +55,8 @@ def tile_moe_res_mlp_gelu_kernel(tc, xT, xr, w1, w2, gate, offs, out):
             nc.vector.memset(sums[b][:], 0.0)
 
         x_codes = [keep.tile([P, T], U32, name=f"x_codes{s}", align_bytes=64) for s in range(PASSES)]
-        g_codes = [
-            [keep.tile([P, LIST_HALF], U32, name=f"g_codes{s}_{f}", align_bytes=64) for f in range(2)]
-            for s in range(PASSES)
-        ]
-        g_scales = [keep.tile([P, LIST_HALF], U8, name=f"g_scales{f}", align_bytes=64) for f in range(2)]
+        g_codes = [{} for s in range(PASSES)]
+        g_scales = {}
         gates = {}
         residual = {}
         w2_rows = {}
@@ -129,17 +127,20 @@ def tile_moe_res_mlp_gelu_kernel(tc, xT, xr, w1, w2, gate, offs, out):
                 src = loaded[item][:].rearrange("p j (m t) -> p m j t", t=4)
                 if b == 0:
                     grouped[item] = stage.tile([P, 4 * H], BF16, name="wide", align_bytes=64)
-                    wide = grouped[item][:]
-                elif b == 1:
-                    grouped[item] = pair_stage.tile([P, 8 * H], BF16, name="pair", align_bytes=64)
-                    wide = grouped[item][:, 0 : 4 * H]
-                else:
-                    wide = grouped["w1", a, 1][:, 4 * H : 8 * H]
-                dst = wide.rearrange("p (t m j) -> p m j t", t=4, j=4)
-                if b == PASSES - 1 and a > 0:
-                    nc.vector.tensor_copy(out=dst, in_=src)
-                else:
-                    nc.scalar.copy(out=dst, in_=src)
+                    nc.scalar.copy(out=grouped[item][:].rearrange("p (t m j) -> p m j t", t=4, j=4), in_=src)
+                    return
+                for half in (1, 0):
+                    if b == 1 and a == 0 and half == 0:
+                        grouped[a, half] = shared.tile([P, 4 * H], BF16, name="first_pair", align_bytes=64, offset=0)
+                    elif b == 1:
+                        grouped[a, half] = pair_stage.tile([P, 4 * H], BF16, name=f"pair{half}", align_bytes=64)
+                    wide = grouped[a, half][:, 2 * H * (b - 1) : 2 * H * b]
+                    on_vector = (b == 2 and a > 0) or (item == ("w1", 1, 1) and half == 1)
+                    copy = nc.vector.tensor_copy if on_vector else nc.scalar.copy
+                    copy(
+                        out=wide.rearrange("p (t m j) -> p m j t", t=2, j=4),
+                        in_=src[:, :, :, 2 * half : 2 * half + 2],
+                    )
             elif kind == "x":
                 c0, width = X_CHUNKS[b]
                 engine = "V" if b == 1 or (b == 2 and a == PASSES - 1) else "S"
@@ -148,7 +149,7 @@ def tile_moe_res_mlp_gelu_kernel(tc, xT, xr, w1, w2, gate, offs, out):
                 grouped[item] = wide
             else:
                 wide = stage.tile([P, 4 * N], BF16, name="wide", align_bytes=64)
-                side_by_side("S", wide[:], w2_rows[a][:])
+                side_by_side("V" if a == 0 else "S", wide[:], w2_rows[a][:])
                 grouped[item] = wide
 
         def quantize(item):
@@ -165,42 +166,60 @@ def tile_moe_res_mlp_gelu_kernel(tc, xT, xr, w1, w2, gate, offs, out):
                     scales = w_pool.tile([P, PASSES * H], U8, name="w1_scales", align_bytes=64)
                     weights[a] = (codes, scales)
                 codes, scales = weights[a]
-                if b != 1:
-                    cols = slice(0, H) if b == 0 else slice(H, PASSES * H)
-                    wide = grouped.pop(("w1", a, min(b, 1)))
+                if b == 0:
+                    pieces = [(0, grouped.pop(item))]
+                else:
+                    pieces = [(H * (1 + half), grouped.pop((a, half))) for half in (1, 0) if b == 2]
+                for c0, wide in pieces:
+                    cols = slice(c0, c0 + H)
                     nc.vector.quantize_mx(out=codes[:, cols].bitcast(FP8X4), scales=scales[:, cols], in_=wide[:])
             else:
                 nc.vector.quantize_mx(
                     out=w2_codes[a][:].bitcast(FP8X4), scales=w2_scales[a][:], in_=grouped.pop(item)[:]
                 )
 
-        def gather(target, window, f):
-            nc.vector.tensor_copy(target[f][:], window[:].indirect(offsets[:, 32 * f : 32 * (f + 1)]))
+        def gather(s, f):
+            late = f == 1 and s == PASSES - 1
+            jobs = [(g_codes[s], x_codes[s], U32, f"g_codes{s}_{f}", 0)]
+            if s == PASSES - 1:
+                jobs.append((g_scales, x_scales, U8, f"g_scales{f}", 4 * LIST_HALF))
+            for target, window, dtype, name, at in jobs:
+                if late:
+                    target[f] = shared.tile([P, LIST_HALF], dtype, name=name, align_bytes=64, offset=at)
+                else:
+                    target[f] = keep.tile([P, LIST_HALF], dtype, name=name, align_bytes=64)
+                nc.vector.tensor_copy(target[f][:], window[:].indirect(offsets[:, 32 * f : 32 * (f + 1)]))
 
-        def first_layer(e, part):
-            f, at = divmod(C * e + P * part, LIST_HALF)
-            a_bank = psum1.tile([P, 4, P], F32, name="a_bank")
-            for t in range(4):
-                for s in range(PASSES):
-                    rows = slice(H * s + P * t, H * s + P * (t + 1))
-                    codes, scales = weights[e]
-                    nc.tensor.matmul_mx(
-                        out=a_bank[:, t, :],
-                        lhsT=codes[:, rows].bitcast(FP8X4),
-                        lhsT_scale=scales[:, rows],
-                        rhs=g_codes[s][f][:, at : at + P].bitcast(FP8X4),
-                        rhs_scale=g_scales[f][4 * s : P, at : at + P],
-                        start=(s == 0),
-                        stop=(s == PASSES - 1),
-                    )
-            if part == 0 and e < E - 1:
+        def first_layer(e):
+            a_banks = [psum1.tile([P, 4, P], F32, name="a_bank") for part in range(2)]
+            codes, scales = weights[e]
+            for half in (1, 0):
+                for part in range(2):
+                    f, at = divmod(C * e + P * part, LIST_HALF)
+                    for t in range(2 * half, 2 * half + 2):
+                        for s in range(PASSES):
+                            c0 = P * t if s == 0 else H * (1 + half) + 2 * P * (s - 1) + P * (t % 2)
+                            rows = slice(c0, c0 + P)
+                            nc.tensor.matmul_mx(
+                                out=a_banks[part][:, t, :],
+                                lhsT=codes[:, rows].bitcast(FP8X4),
+                                lhsT_scale=scales[:, rows],
+                                rhs=g_codes[s][f][:, at : at + P].bitcast(FP8X4),
+                                rhs_scale=g_scales[f][4 * s : P, at : at + P],
+                                start=(s == 0),
+                                stop=(s == PASSES - 1),
+                            )
+            if e < E - 1:
                 hidden[e] = loaded["w1", e + 1, 0][:, 0, :].bitcast(BF16)
-            elif part == 0:
+            else:
                 hidden[e] = small.tile([P, 4 * C], BF16, name="h", align_bytes=64)[:]
-            h = hidden[e][:, 4 * P * part : 4 * P * (part + 1)]
-            nc.scalar.activation(
-                out=h.rearrange("p (n t) -> p n t", t=4), in_=a_bank[:].rearrange("p t n -> p n t"), func=GELU
-            )
+            for part in range(2):
+                h = hidden[e][:, 4 * P * part : 4 * P * (part + 1)]
+                nc.scalar.activation(
+                    out=h.rearrange("p (n t) -> p n t", t=4),
+                    in_=a_banks[part][:].rearrange("p t n -> p n t"),
+                    func=GELU,
+                )
 
         def second_layer(e):
             h_codes = small.tile([P, C], U32, name="h_codes", align_bytes=64)
@@ -244,7 +263,7 @@ def tile_moe_res_mlp_gelu_kernel(tc, xT, xr, w1, w2, gate, offs, out):
             )
 
         def finish(b):
-            for c0, c1 in ((0, T),) if b == 0 else ((0, 896), (896, T)):
+            for c0, c1 in ((0, 640), (640, T)) if b == 0 else ((0, 512), (512, 1024), (1024, T)):
                 cols = slice(c0, c1)
                 nc.vector.tensor_tensor(residual[b][:, cols], sums[b][:, cols], residual[b][:, cols], ADD)
                 nc.sync.dma_start(out=out[P * b : P * (b + 1), cols], in_=residual[b][:, cols])
@@ -261,16 +280,15 @@ def tile_moe_res_mlp_gelu_kernel(tc, xT, xr, w1, w2, gate, offs, out):
                 item = items[step - 1]
                 quantize(item)
                 if item[0] == "x" and item[2] == len(X_CHUNKS) - 1:
-                    s = item[1]
-                    for f in range(2):
-                        gather(g_codes[s], x_codes[s], f)
-                        if s == PASSES - 1:
-                            gather(g_scales, x_scales, f)
+                    gather(item[1], 0)
+                    if item[1] < PASSES - 1:
+                        gather(item[1], 1)
+                if item == ("w2", 0, 0):
+                    gather(PASSES - 1, 1)
             for e in range(E):
                 lag = step - last_w1[e]
                 if lag == 2:
-                    first_layer(e, 0)
-                    first_layer(e, 1)
+                    first_layer(e)
                 if lag == 3:
                     second_layer(e)
                 if lag == 5:

@@ -1,12 +1,13 @@
 from contextlib import ExitStack
 
 import concourse.mybir as mybir
+from concourse.masks import make_identity
 
 K, T, E, C, H, N = 1536, 1280, 4, 256, 512, 256
 S = E * C
 
 FLOPS = 2 * S * K * H + 2 * S * H * N
-BYTES = 4 * (K * T + 2 * N * T + E * K * H + E * H * N + 128 * S) + 2 * 128 * (S // 16)
+BYTES = 4 * (K * T + 2 * N * T + E * K * H + E * H * N + S) + 2 * 128 * (S // 16)
 
 F32 = mybir.dt.float32
 BF16 = mybir.dt.bfloat16
@@ -57,7 +58,20 @@ def tile_moe_res_mlp_gelu_kernel(tc, xT, xr, w1, w2, gate, offs, out):
         x_codes = [keep.tile([P, T], U32, name=f"x_codes{s}", align_bytes=64) for s in range(PASSES)]
         g_codes = [{} for s in range(PASSES)]
         g_scales = {}
-        gates = {}
+        identity = keep.tile([P, P], F32, name="identity")
+        make_identity(nc, identity[:])
+        gate_rows = keep.tile([P, 8], F32, name="gate_rows")
+        nc.scalar.dma_start(out=gate_rows[:], in_=gate[0:1, :].rearrange("o (p c) -> (o p) c", c=8))
+        gates = keep.tile([P, S], F32, name="gates")
+        for half in range(2):
+            spread = psum1.tile([P, 4, P], F32, name="a_bank")
+            for c in range(4):
+                column = gate_rows[:, 4 * half + c : 4 * half + c + 1]
+                nc.tensor.transpose(spread[:, c, :], column.to_broadcast([P, P]), identity[:])
+            nc.scalar.copy(
+                out=gates[:].rearrange("p (n c) -> p n c", c=8)[:, :, 4 * half : 4 * half + 4],
+                in_=spread[:].rearrange("p c n -> p n c"),
+            )
         residual = {}
         w2_rows = {}
         w2_codes = [keep.tile([P, N], U32, name=f"w2_codes{e}", align_bytes=64) for e in range(E)]
@@ -79,10 +93,6 @@ def tile_moe_res_mlp_gelu_kernel(tc, xT, xr, w1, w2, gate, offs, out):
             )
             return slots[-1]
 
-        def load_gates(f):
-            gates[f] = slot([P, LIST_HALF])
-            nc.sync.dma_start(out=gates[f][:], in_=gate[0:P, LIST_HALF * f : LIST_HALF * (f + 1)])
-
         def load(item):
             kind, a, b = item
             if kind == "x":
@@ -97,12 +107,9 @@ def tile_moe_res_mlp_gelu_kernel(tc, xT, xr, w1, w2, gate, offs, out):
                 rows = w1[a, 512 * b : 512 * (b + 1), :]
                 nc.sync.dma_start(out=loaded[item][:], in_=rows.rearrange("(p j) w -> p j w", j=4))
             else:
-                if a == 1:
-                    load_gates(0)
                 w2_rows[a] = slot([P, 4, N])
                 nc.sync.dma_start(out=w2_rows[a][:], in_=w2[a].rearrange("(p j) w -> p j w", j=4))
                 if a == E - 1:
-                    load_gates(1)
                     for c in range(2):
                         residual[c] = slot([P, T])
                         nc.sync.dma_start(out=residual[c][:], in_=xr[P * c : P * (c + 1), :])
@@ -135,7 +142,7 @@ def tile_moe_res_mlp_gelu_kernel(tc, xT, xr, w1, w2, gate, offs, out):
                     elif b == 1:
                         grouped[a, half] = pair_stage.tile([P, 4 * H], BF16, name=f"pair{half}", align_bytes=64)
                     wide = grouped[a, half][:, 2 * H * (b - 1) : 2 * H * b]
-                    on_vector = (b == 2 and a > 0) or (item == ("w1", 1, 1) and half == 1)
+                    on_vector = a > 0 and (b == 2 or half == 1)
                     copy = nc.vector.tensor_copy if on_vector else nc.scalar.copy
                     copy(
                         out=wide.rearrange("p (t m j) -> p m j t", t=2, j=4),
@@ -149,7 +156,7 @@ def tile_moe_res_mlp_gelu_kernel(tc, xT, xr, w1, w2, gate, offs, out):
                 grouped[item] = wide
             else:
                 wide = stage.tile([P, 4 * N], BF16, name="wide", align_bytes=64)
-                side_by_side("V" if a == 0 else "S", wide[:], w2_rows[a][:])
+                side_by_side("S", wide[:], w2_rows[a][:])
                 grouped[item] = wide
 
         def quantize(item):
@@ -240,9 +247,7 @@ def tile_moe_res_mlp_gelu_kernel(tc, xT, xr, w1, w2, gate, offs, out):
             banks[e] = y_bank
 
         def leave_bank(e):
-            if e < E - 2:
-                y = w2_rows[e + 1][:, 0:2, :]
-            elif e == E - 2:
+            if e < E - 1:
                 y = loaded["w1", e + 1, 1][:, 0, :].rearrange("p (b n) -> p b n", b=2)
             else:
                 y = small.tile([P, 2, C], F32, name="y")[:]
@@ -254,11 +259,10 @@ def tile_moe_res_mlp_gelu_kernel(tc, xT, xr, w1, w2, gate, offs, out):
             results[e] = y
 
         def put_back(e, b):
-            f, at = divmod(C * e, LIST_HALF)
             nc.vector.tensor_tensor(
                 sums[b][:].indirect(offsets[:, 16 * e : 16 * (e + 1)]),
                 results[e][:, b, :],
-                gates[f][:, at : at + C],
+                gates[:, C * e : C * (e + 1)],
                 MULT,
             )
 
@@ -291,7 +295,7 @@ def tile_moe_res_mlp_gelu_kernel(tc, xT, xr, w1, w2, gate, offs, out):
                     first_layer(e)
                 if lag == 3:
                     second_layer(e)
-                if lag == 5:
+                if lag == 4:
                     leave_bank(e)
                 if lag == 6:
                     for b in range(2):

@@ -26,6 +26,7 @@ LIST_HALF = 512
 X_CHUNKS = ((0, 512), (512, 512), (1024, 256))
 SLOT = 4 * H * 4
 SLOTS = 15
+QUARTER = {(1, 0): 0, (2, 0): 1, (2, 1): 2, (1, 1): 3}
 X_BYTES = 4 * T * 4
 FIRST_FREE = 8
 
@@ -136,18 +137,18 @@ def tile_moe_res_mlp_gelu_kernel(tc, xT, xr, w1, w2, gate, offs, out):
                     grouped[item] = stage.tile([P, 4 * H], BF16, name="wide", align_bytes=64)
                     nc.scalar.copy(out=grouped[item][:].rearrange("p (t m j) -> p m j t", t=4, j=4), in_=src)
                     return
-                for half in (1, 0):
-                    if b == 1 and a == 0 and half == 0:
-                        grouped[a, half] = shared.tile([P, 4 * H], BF16, name="first_pair", align_bytes=64, offset=0)
-                    elif b == 1:
-                        grouped[a, half] = pair_stage.tile([P, 4 * H], BF16, name=f"pair{half}", align_bytes=64)
-                    wide = grouped[a, half][:, 2 * H * (b - 1) : 2 * H * b]
-                    on_vector = a > 0 and (b == 2 or half == 1)
-                    copy = nc.vector.tensor_copy if on_vector else nc.scalar.copy
-                    copy(
-                        out=wide.rearrange("p (t m j) -> p m j t", t=2, j=4),
-                        in_=src[:, :, :, 2 * half : 2 * half + 2],
-                    )
+                if b == 1 and a == 0:
+                    grouped[a] = shared.tile([P, 8 * H], BF16, name="first_pair", align_bytes=64, offset=0)
+                elif b == 1:
+                    grouped[a] = pair_stage.tile([P, 8 * H], BF16, name="pair", align_bytes=64)
+                if a > 0 and b == 2:
+                    dst = grouped[a][:, 2 * H : 6 * H].rearrange("p (t m j) -> p m j t", t=4, j=4)
+                    nc.vector.tensor_copy(out=dst, in_=src)
+                    return
+                for half in range(2):
+                    at = 2 * H * QUARTER[b, half]
+                    dst = grouped[a][:, at : at + 2 * H].rearrange("p (t m j) -> p m j t", t=2, j=4)
+                    nc.scalar.copy(out=dst, in_=src[:, :, :, 2 * half : 2 * half + 2])
             elif kind == "x":
                 c0, width = X_CHUNKS[b]
                 engine = "V" if b == 1 or (b == 2 and a == PASSES - 1) else "S"
@@ -156,7 +157,7 @@ def tile_moe_res_mlp_gelu_kernel(tc, xT, xr, w1, w2, gate, offs, out):
                 grouped[item] = wide
             else:
                 wide = stage.tile([P, 4 * N], BF16, name="wide", align_bytes=64)
-                side_by_side("S", wide[:], w2_rows[a][:])
+                side_by_side("V" if 0 < a < E - 1 else "S", wide[:], w2_rows[a][:])
                 grouped[item] = wide
 
         def quantize(item):
@@ -174,12 +175,16 @@ def tile_moe_res_mlp_gelu_kernel(tc, xT, xr, w1, w2, gate, offs, out):
                     weights[a] = (codes, scales)
                 codes, scales = weights[a]
                 if b == 0:
-                    pieces = [(0, grouped.pop(item))]
+                    pieces = [(0, grouped.pop(item)[:])]
                 else:
-                    pieces = [(H * (1 + half), grouped.pop((a, half))) for half in (1, 0) if b == 2]
+                    pieces = [
+                        (H * (1 + half), grouped[a][:, 4 * H * half : 4 * H * (half + 1)])
+                        for half in range(2)
+                        if b == 2
+                    ]
                 for c0, wide in pieces:
                     cols = slice(c0, c0 + H)
-                    nc.vector.quantize_mx(out=codes[:, cols].bitcast(FP8X4), scales=scales[:, cols], in_=wide[:])
+                    nc.vector.quantize_mx(out=codes[:, cols].bitcast(FP8X4), scales=scales[:, cols], in_=wide)
             else:
                 nc.vector.quantize_mx(
                     out=w2_codes[a][:].bitcast(FP8X4), scales=w2_scales[a][:], in_=grouped.pop(item)[:]
@@ -200,12 +205,12 @@ def tile_moe_res_mlp_gelu_kernel(tc, xT, xr, w1, w2, gate, offs, out):
         def first_layer(e):
             a_banks = [psum1.tile([P, 4, P], F32, name="a_bank") for part in range(2)]
             codes, scales = weights[e]
-            for half in (1, 0):
+            for half in range(2):
                 for part in range(2):
                     f, at = divmod(C * e + P * part, LIST_HALF)
                     for t in range(2 * half, 2 * half + 2):
                         for s in range(PASSES):
-                            c0 = P * t if s == 0 else H * (1 + half) + 2 * P * (s - 1) + P * (t % 2)
+                            c0 = P * t if s == 0 else H + 2 * P * QUARTER[s, half] + P * (t % 2)
                             rows = slice(c0, c0 + P)
                             nc.tensor.matmul_mx(
                                 out=a_banks[part][:, t, :],

@@ -41,7 +41,7 @@ def tile_moe_res_mlp_gelu_kernel(tc, xT, xr, w1, w2, gate, offs, out):
         pair_stage = ctx.enter_context(tc.tile_pool(name="pair_stage", bufs=1))
         w_pool = ctx.enter_context(tc.tile_pool(name="w_pool", bufs=2))
         small = ctx.enter_context(tc.tile_pool(name="small", bufs=3))
-        psum1 = ctx.enter_context(tc.psum_pool(name="psum1", bufs=4))
+        psum1 = ctx.enter_context(tc.psum_pool(name="psum1", bufs=2))
         psum2 = ctx.enter_context(tc.psum_pool(name="psum2", bufs=3))
 
         offsets = keep.tile([P, S // 16], U16, name="offsets")
@@ -80,7 +80,8 @@ def tile_moe_res_mlp_gelu_kernel(tc, xT, xr, w1, w2, gate, offs, out):
 
         items = [("x", s, chunk) for s in range(PASSES) for chunk in range(len(X_CHUNKS))]
         for e in range(E):
-            items += [("w1", e, s) for s in range(PASSES)] + [("w2", e, 0)]
+            items += [("w1", e, s) for s in range(PASSES)]
+            items += [("w2", late, 0) for late in ((0,), (1,), (), (2, 3))[e]]
         last_w1 = [items.index(("w1", e, PASSES - 1)) for e in range(E)]
         loaded = {}
         slots = []
@@ -157,7 +158,7 @@ def tile_moe_res_mlp_gelu_kernel(tc, xT, xr, w1, w2, gate, offs, out):
                 grouped[item] = wide
             else:
                 wide = stage.tile([P, 4 * N], BF16, name="wide", align_bytes=64)
-                side_by_side("V" if 0 < a < E - 1 else "S", wide[:], w2_rows[a][:])
+                side_by_side("V" if a == 1 else "S", wide[:], w2_rows[a][:])
                 grouped[item] = wide
 
         def quantize(item):
@@ -233,15 +234,22 @@ def tile_moe_res_mlp_gelu_kernel(tc, xT, xr, w1, w2, gate, offs, out):
                     func=GELU,
                 )
 
-        def second_layer(e):
+        def quantize_hidden(e):
             h_codes = small.tile([P, C], U32, name="h_codes", align_bytes=64)
             h_scales = small.tile([P, C], U8, name="h_scales", align_bytes=64)
             nc.vector.quantize_mx(out=h_codes[:].bitcast(FP8X4), scales=h_scales[:], in_=hidden[e])
-            y_bank = psum2.tile([P, 2, C], F32, name="y_bank")
-            for b in range(2):
+            hidden[e] = (h_codes, h_scales)
+
+        def second_layer(e, blocks):
+            h_codes, h_scales = hidden[e]
+            if (e, blocks) == (E - 2, (1,)):
+                bank = psum1.tile([P, 2, C], F32, name="a_bank")
+            else:
+                bank = psum2.tile([P, 2, C], F32, name="y_bank")
+            for b in blocks:
                 rows = slice(P * b, P * (b + 1))
                 nc.tensor.matmul_mx(
-                    out=y_bank[:, b, :],
+                    out=bank[:, b, :],
                     lhsT=w2_codes[e][:, rows].bitcast(FP8X4),
                     lhsT_scale=w2_scales[e][:, rows],
                     rhs=h_codes[:].bitcast(FP8X4),
@@ -249,19 +257,17 @@ def tile_moe_res_mlp_gelu_kernel(tc, xT, xr, w1, w2, gate, offs, out):
                     start=True,
                     stop=True,
                 )
-            banks[e] = y_bank
+                banks[e, b] = bank
 
-        def leave_bank(e):
-            if e < E - 1:
-                y = loaded["w1", e + 1, 1][:, 0, :].rearrange("p (b n) -> p b n", b=2)
-            else:
-                y = small.tile([P, 2, C], F32, name="y")[:]
-            if e < E - 1:
-                nc.scalar.copy(out=y, in_=banks[e][:])
-            else:
-                for b in range(2):
-                    nc.scalar.copy(out=y[:, b, :], in_=banks[e][:, b, :])
-            results[e] = y
+        def leave_bank(e, blocks):
+            if e < E - 2:
+                results[e] = loaded["w1", e + 1, 1][:, 0, :].rearrange("p (b n) -> p b n", b=2)
+                nc.scalar.copy(out=results[e], in_=banks[e, 0][:])
+                return
+            if e not in results:
+                results[e] = small.tile([P, 2, C], F32, name="y")[:]
+            for b in blocks:
+                nc.scalar.copy(out=results[e][:, b, :], in_=banks[e, b][:, b, :])
 
         def put_back(e, b):
             nc.vector.tensor_tensor(
@@ -280,12 +286,11 @@ def tile_moe_res_mlp_gelu_kernel(tc, xT, xr, w1, w2, gate, offs, out):
         ahead = 12
         for item in items[:ahead]:
             load(item)
-        for step in range(len(items) + 7):
-            if step < len(items):
-                interleave(items[step])
+        for step in range(len(items) - 1):
+            interleave(items[step])
             if step + ahead < len(items):
                 load(items[step + ahead])
-            if 1 <= step <= len(items):
+            if step >= 1:
                 item = items[step - 1]
                 quantize(item)
                 if item[0] == "x" and item[2] == len(X_CHUNKS) - 1:
@@ -294,16 +299,31 @@ def tile_moe_res_mlp_gelu_kernel(tc, xT, xr, w1, w2, gate, offs, out):
                         gather(item[1], 1)
                 if item == ("w2", 0, 0):
                     gather(PASSES - 1, 1)
-            for e in range(E):
-                lag = step - last_w1[e]
-                if lag == 2:
+            for e in range(E - 1):
+                if items[step] == ("w1", e + 1, 0):
                     first_layer(e)
-                if lag == 3:
-                    second_layer(e)
-                if lag == 4:
-                    leave_bank(e)
-                if lag == 6:
-                    for b in range(2):
-                        put_back(e, b)
-                        if e == E - 1:
-                            finish(b)
+                if items[step] == ("w1", e + 1, 1):
+                    quantize_hidden(e)
+                    if e < E - 2:
+                        second_layer(e, (0, 1))
+                if items[step] == ("w1", e + 1, 2) and e < E - 2:
+                    leave_bank(e, (0, 1))
+                if items[step] == ("w1", e + 2, 0):
+                    put_back(e, 0)
+                    put_back(e, 1)
+        quantize(("w2", E - 2, 0))
+        second_layer(E - 2, (0,))
+        leave_bank(E - 2, (0,))
+        interleave(("w2", E - 1, 0))
+        quantize(("w2", E - 1, 0))
+        put_back(E - 2, 0)
+        first_layer(E - 1)
+        quantize_hidden(E - 1)
+        second_layer(E - 2, (1,))
+        leave_bank(E - 2, (1,))
+        put_back(E - 2, 1)
+        second_layer(E - 1, (0, 1))
+        leave_bank(E - 1, (0, 1))
+        for b in range(2):
+            put_back(E - 1, b)
+            finish(b)

@@ -26,9 +26,14 @@ LIST_HALF = 512
 X_CHUNKS = ((0, 512), (512, 512), (1024, 256))
 SLOT = 4 * H * 4
 SLOTS = 15
-QUARTER = {(1, 0): 0, (2, 0): 1, (2, 1): 2, (1, 1): 3}
 X_BYTES = 4 * T * 4
 FIRST_FREE = 8
+V_PASS = (2, 1, 1, 1)
+V_W2 = (1,2)
+V_X = ((1,2),(1,),(1,))
+H3 = 1
+SPLIT = (3,)
+Y_AT = 2
 
 
 def tile_moe_res_mlp_gelu_kernel(tc, xT, xr, w1, w2, gate, offs, out):
@@ -36,9 +41,8 @@ def tile_moe_res_mlp_gelu_kernel(tc, xT, xr, w1, w2, gate, offs, out):
     with ExitStack() as ctx:
         keep = ctx.enter_context(tc.tile_pool(name="keep", bufs=1))
         rows_pool = ctx.enter_context(tc.tile_pool(name="rows_pool", bufs=1))
-        stage = ctx.enter_context(tc.tile_pool(name="stage", bufs=4))
+        stage = ctx.enter_context(tc.tile_pool(name="stage", bufs=6))
         shared = ctx.enter_context(tc.tile_pool(name="shared", bufs=1))
-        pair_stage = ctx.enter_context(tc.tile_pool(name="pair_stage", bufs=1))
         w_pool = ctx.enter_context(tc.tile_pool(name="w_pool", bufs=2))
         small = ctx.enter_context(tc.tile_pool(name="small", bufs=3))
         psum1 = ctx.enter_context(tc.psum_pool(name="psum1", bufs=2))
@@ -81,19 +85,19 @@ def tile_moe_res_mlp_gelu_kernel(tc, xT, xr, w1, w2, gate, offs, out):
         items = [("x", s, chunk) for s in range(PASSES) for chunk in range(len(X_CHUNKS))]
         for e in range(E):
             items += [("w1", e, s) for s in range(PASSES)]
-            items += [("w2", late, 0) for late in ((0,), (1,), (), (2, 3))[e]]
+            items += [("w2", late, 0) for late in (e,)]
         last_w1 = [items.index(("w1", e, PASSES - 1)) for e in range(E)]
         loaded = {}
-        slots = []
 
-        def slot(shape):
-            number = len(slots)
-            slots.append(
-                rows_pool.tile(
-                    shape, F32, name=f"rows{number}", align_bytes=64, offset=SLOT * ((FIRST_FREE + number) % SLOTS)
-                )
-            )
-            return slots[-1]
+        place = {}
+
+        def slot(item, shape):
+            place[item] = SLOT * ((FIRST_FREE + len(place)) % SLOTS)
+            return over(item, 0, shape, F32, "rows")
+
+        def over(item, at, shape, dtype, what):
+            name = what + "".join(f"_{part}" for part in item)
+            return rows_pool.tile(shape, dtype, name=name, align_bytes=64, offset=place[item] + at)
 
         def load(item):
             kind, a, b = item
@@ -102,24 +106,25 @@ def tile_moe_res_mlp_gelu_kernel(tc, xT, xr, w1, w2, gate, offs, out):
                     loaded[a] = rows_pool.tile([P, 4, T], F32, name=f"x_rows{a}", align_bytes=64, offset=X_BYTES * a)
                     rows = xT[512 * a : 512 * (a + 1), :]
                     nc.sync.dma_start(out=loaded[a][:], in_=rows.rearrange("(p j) w -> p j w", j=4))
-                if item == ("x", 1, 0):
+                if item == ("x", 0, 0):
                     nc.sync.dma_start(offsets[:], offs)
             elif kind == "w1":
-                loaded[item] = slot([P, 4, H])
+                loaded[item] = slot(item, [P, 4, H])
                 rows = w1[a, 512 * b : 512 * (b + 1), :]
                 nc.sync.dma_start(out=loaded[item][:], in_=rows.rearrange("(p j) w -> p j w", j=4))
             else:
-                w2_rows[a] = slot([P, 4, N])
+                w2_rows[a] = slot(item, [P, 4, N])
                 nc.sync.dma_start(out=w2_rows[a][:], in_=w2[a].rearrange("(p j) w -> p j w", j=4))
                 if a == E - 1:
                     for c in range(2):
-                        residual[c] = slot([P, T])
+                        residual[c] = slot(("xr", c, 0), [P, T])
                         nc.sync.dma_start(out=residual[c][:], in_=xr[P * c : P * (c + 1), :])
 
         grouped = {}
         weights = {}
         hidden = {}
         banks = {}
+        a_banks = {}
         results = {}
 
         def side_by_side(engine, dst, src):
@@ -134,31 +139,36 @@ def tile_moe_res_mlp_gelu_kernel(tc, xT, xr, w1, w2, gate, offs, out):
             kind, a, b = item
             if kind == "w1":
                 src = loaded[item][:].rearrange("p j (m t) -> p m j t", t=4)
-                if b == 0:
+                if (a, b) == (0, PASSES - 1):
+                    grouped[item] = shared.tile([P, 4 * H], BF16, name="first_last", align_bytes=64, offset=0)
+                elif a > 0 and b == 1:
+                    grouped[item] = over(("w1", a, 0), SLOT // 2, [P, 4 * H], BF16, "wide")
+                else:
                     grouped[item] = stage.tile([P, 4 * H], BF16, name="wide", align_bytes=64)
-                    nc.scalar.copy(out=grouped[item][:].rearrange("p (t m j) -> p m j t", t=4, j=4), in_=src)
-                    return
-                if b == 1 and a == 0:
-                    grouped[a] = shared.tile([P, 8 * H], BF16, name="first_pair", align_bytes=64, offset=0)
-                elif b == 1:
-                    grouped[a] = pair_stage.tile([P, 8 * H], BF16, name="pair", align_bytes=64)
-                if a > 0 and b == 2:
-                    dst = grouped[a][:, 2 * H : 6 * H].rearrange("p (t m j) -> p m j t", t=4, j=4)
+                dst = grouped[item][:].rearrange("p (t m j) -> p m j t", t=4, j=4)
+                if a in SPLIT and b > 0:
+                    for half, copy in enumerate((nc.vector.tensor_copy, nc.scalar.copy)):
+                        part = grouped[item][:, 2 * H * half : 2 * H * (half + 1)]
+                        copy(
+                            out=part.rearrange("p (t m j) -> p m j t", t=2, j=4),
+                            in_=src[:, :, :, 2 * half : 2 * half + 2],
+                        )
+                elif b == V_PASS[a]:
                     nc.vector.tensor_copy(out=dst, in_=src)
-                    return
-                for half in range(2):
-                    at = 2 * H * QUARTER[b, half]
-                    dst = grouped[a][:, at : at + 2 * H].rearrange("p (t m j) -> p m j t", t=2, j=4)
-                    nc.scalar.copy(out=dst, in_=src[:, :, :, 2 * half : 2 * half + 2])
+                else:
+                    nc.scalar.copy(out=dst, in_=src)
             elif kind == "x":
                 c0, width = X_CHUNKS[b]
-                engine = "V" if b == 1 or (b == 2 and a == PASSES - 1) else "S"
+                engine = "V" if b in V_X[a] else "S"
                 wide = stage.tile([P, 4 * width], BF16, name="wide", align_bytes=64)
                 side_by_side(engine, wide[:], loaded[a][:, :, c0 : c0 + width])
                 grouped[item] = wide
             else:
-                wide = stage.tile([P, 4 * N], BF16, name="wide", align_bytes=64)
-                side_by_side("V" if a == 1 else "S", wide[:], w2_rows[a][:])
+                if a > 0 and a not in V_W2:
+                    wide = over(("w1", a, Y_AT), SLOT // 2, [P, 4 * N], BF16, "wide")
+                else:
+                    wide = stage.tile([P, 4 * N], BF16, name="wide", align_bytes=64)
+                side_by_side("V" if a in V_W2 else "S", wide[:], w2_rows[a][:])
                 grouped[item] = wide
 
         def quantize(item):
@@ -175,17 +185,10 @@ def tile_moe_res_mlp_gelu_kernel(tc, xT, xr, w1, w2, gate, offs, out):
                     scales = w_pool.tile([P, PASSES * H], U8, name="w1_scales", align_bytes=64)
                     weights[a] = (codes, scales)
                 codes, scales = weights[a]
-                if b == 0:
-                    pieces = [(0, grouped.pop(item)[:])]
-                else:
-                    pieces = [
-                        (H * (1 + half), grouped[a][:, 4 * H * half : 4 * H * (half + 1)])
-                        for half in range(2)
-                        if b == 2
-                    ]
-                for c0, wide in pieces:
-                    cols = slice(c0, c0 + H)
-                    nc.vector.quantize_mx(out=codes[:, cols].bitcast(FP8X4), scales=scales[:, cols], in_=wide)
+                cols = slice(H * b, H * (b + 1))
+                nc.vector.quantize_mx(
+                    out=codes[:, cols].bitcast(FP8X4), scales=scales[:, cols], in_=grouped.pop(item)[:]
+                )
             else:
                 nc.vector.quantize_mx(
                     out=w2_codes[a][:].bitcast(FP8X4), scales=w2_scales[a][:], in_=grouped.pop(item)[:]
@@ -203,34 +206,36 @@ def tile_moe_res_mlp_gelu_kernel(tc, xT, xr, w1, w2, gate, offs, out):
                     target[f] = keep.tile([P, LIST_HALF], dtype, name=name, align_bytes=64)
                 nc.vector.tensor_copy(target[f][:], window[:].indirect(offsets[:, 32 * f : 32 * (f + 1)]))
 
-        def first_layer(e):
-            a_banks = [psum1.tile([P, 4, P], F32, name="a_bank") for part in range(2)]
+        def first_layer(e, s):
+            if s == 0:
+                a_banks[e] = [psum1.tile([P, 4, P], F32, name="a_bank") for part in range(2)]
             codes, scales = weights[e]
-            for half in range(2):
-                for part in range(2):
-                    f, at = divmod(C * e + P * part, LIST_HALF)
-                    for t in range(2 * half, 2 * half + 2):
-                        for s in range(PASSES):
-                            c0 = P * t if s == 0 else H + 2 * P * QUARTER[s, half] + P * (t % 2)
-                            rows = slice(c0, c0 + P)
-                            nc.tensor.matmul_mx(
-                                out=a_banks[part][:, t, :],
-                                lhsT=codes[:, rows].bitcast(FP8X4),
-                                lhsT_scale=scales[:, rows],
-                                rhs=g_codes[s][f][:, at : at + P].bitcast(FP8X4),
-                                rhs_scale=g_scales[f][4 * s : P, at : at + P],
-                                start=(s == 0),
-                                stop=(s == PASSES - 1),
-                            )
+            for part in range(2):
+                f, at = divmod(C * e + P * part, LIST_HALF)
+                for t in range(4):
+                    rows = slice(H * s + P * t, H * s + P * (t + 1))
+                    nc.tensor.matmul_mx(
+                        out=a_banks[e][part][:, t, :],
+                        lhsT=codes[:, rows].bitcast(FP8X4),
+                        lhsT_scale=scales[:, rows],
+                        rhs=g_codes[s][f][:, at : at + P].bitcast(FP8X4),
+                        rhs_scale=g_scales[f][4 * s : P, at : at + P],
+                        start=(s == 0 and t == 0),
+                        stop=(s == PASSES - 1 and t == 3),
+                    )
+
+        def activate(e):
             if e < E - 1:
-                hidden[e] = loaded["w1", e + 1, 0][:, 0, :].bitcast(BF16)
+                hidden[e] = over(("w1", e + 1, 0), 0, [P, 4 * C], BF16, "h")[:]
+            elif H3:
+                hidden[e] = over(("w2", e, 0), 0, [P, 4 * C], BF16, "h")[:]
             else:
                 hidden[e] = small.tile([P, 4 * C], BF16, name="h", align_bytes=64)[:]
             for part in range(2):
                 h = hidden[e][:, 4 * P * part : 4 * P * (part + 1)]
                 nc.scalar.activation(
                     out=h.rearrange("p (n t) -> p n t", t=4),
-                    in_=a_banks[part][:].rearrange("p t n -> p n t"),
+                    in_=a_banks[e][part][:].rearrange("p t n -> p n t"),
                     func=GELU,
                 )
 
@@ -260,19 +265,22 @@ def tile_moe_res_mlp_gelu_kernel(tc, xT, xr, w1, w2, gate, offs, out):
                 banks[e, b] = bank
 
         def leave_bank(e, blocks):
-            if e < E - 2:
-                results[e] = loaded["w1", e + 1, 1][:, 0, :].rearrange("p (b n) -> p b n", b=2)
-                nc.scalar.copy(out=results[e], in_=banks[e, 0][:])
+            if e < E - 2 and len(blocks) == 2:
+                both = over(("w1", e + 1, Y_AT), 0, [P, 2, C], F32, "y")
+                nc.scalar.copy(out=both[:], in_=banks[e, 0][:])
+                results[e, 0], results[e, 1] = both[:, 0, :], both[:, 1, :]
                 return
-            if e not in results:
-                results[e] = small.tile([P, 2, C], F32, name="y")[:]
             for b in blocks:
-                nc.scalar.copy(out=results[e][:, b, :], in_=banks[e, b][:, b, :])
+                if (e, b) == (E - 2, 0):
+                    results[e, b] = over(("w1", e + 1, Y_AT), 0, [P, C], F32, "y")[:]
+                else:
+                    results[e, b] = small.tile([P, C], F32, name=f"y{b}")[:]
+                nc.scalar.copy(out=results[e, b], in_=banks[e, b][:, b, :])
 
         def put_back(e, b):
             nc.vector.tensor_tensor(
                 sums[b][:].indirect(offsets[:, 16 * e : 16 * (e + 1)]),
-                results[e][:, b, :],
+                results[e, b],
                 gates[:, C * e : C * (e + 1)],
                 MULT,
             )
@@ -297,27 +305,27 @@ def tile_moe_res_mlp_gelu_kernel(tc, xT, xr, w1, w2, gate, offs, out):
                     gather(item[1], 0)
                     if item[1] < PASSES - 1:
                         gather(item[1], 1)
+                if item[0] == "w1":
+                    first_layer(item[1], item[2])
                 if item == ("w2", 0, 0):
                     gather(PASSES - 1, 1)
             for e in range(E - 1):
                 if items[step] == ("w1", e + 1, 0):
-                    first_layer(e)
+                    activate(e)
                 if items[step] == ("w1", e + 1, 1):
                     quantize_hidden(e)
-                    if e < E - 2:
-                        second_layer(e, (0, 1))
-                if items[step] == ("w1", e + 1, 2) and e < E - 2:
-                    leave_bank(e, (0, 1))
+                    second_layer(e, (0, 1) if e < E - 2 else (0,))
+                if items[step] == ("w1", e + 1, 2):
+                    leave_bank(e, (0, 1) if e < E - 2 else (0,))
                 if items[step] == ("w1", e + 2, 0):
                     put_back(e, 0)
                     put_back(e, 1)
-        quantize(("w2", E - 2, 0))
-        second_layer(E - 2, (0,))
-        leave_bank(E - 2, (0,))
+        quantize(("w1", E - 1, PASSES - 1))
+        first_layer(E - 1, PASSES - 1)
+        put_back(E - 2, 0)
         interleave(("w2", E - 1, 0))
         quantize(("w2", E - 1, 0))
-        put_back(E - 2, 0)
-        first_layer(E - 1)
+        activate(E - 1)
         quantize_hidden(E - 1)
         second_layer(E - 2, (1,))
         leave_bank(E - 2, (1,))

@@ -128,8 +128,8 @@ def tile_moe_res_mlp_gelu_kernel(tc, xT, xr, w1, w2, gate, offs, out):
         results = {}
 
         def side_by_side(engine, dst, src):
-            dst = dst.rearrange("p (c i j) -> p c j i", i=4, j=4)
-            src = src.rearrange("p j (c i) -> p c j i", i=4)
+            dst = dst.rearrange("p (c i j) -> p c j i", i=2, j=4)
+            src = src.rearrange("p j (c i) -> p c j i", i=2)
             if engine == "V":
                 nc.vector.tensor_copy(out=dst, in_=src)
             else:
@@ -156,7 +156,12 @@ def tile_moe_res_mlp_gelu_kernel(tc, xT, xr, w1, w2, gate, offs, out):
                 elif b == V_PASS[a]:
                     nc.vector.tensor_copy(out=dst, in_=src)
                 else:
-                    nc.scalar.copy(out=dst, in_=src)
+                    for half in range(2):
+                        part = grouped[item][:, 2 * H * half : 2 * H * (half + 1)]
+                        nc.scalar.copy(
+                            out=part.rearrange("p (t m j) -> p m j t", t=2, j=4),
+                            in_=src[:, :, :, 2 * half : 2 * half + 2],
+                        )
             elif kind == "x":
                 c0, width = X_CHUNKS[b]
                 engine = "V" if b in V_X[a] else "S"

@@ -23,15 +23,20 @@ ADD = mybir.AluOpType.add
 P = 128
 PASSES = K // 512
 LIST_HALF = 512
+WINDOW = 1408
 X_CHUNKS = ((0, 512), (512, 512), (1024, 256))
 SLOT = 4 * H * 4
 SLOTS = 15
 X_BYTES = 4 * T * 4
 FIRST_FREE = 8
-V_PASS = (2, 1, 1, 1)
+V_PASS = (1, 1, 1, 1)
 V_W2 = (1,2)
 V_X = ((1,2),(1,),(1,))
-H3 = 1
+H3 = 0
+W2_AT = ((0, 2), (1, 2), (2, 2), (3, 2))
+PARTS = 0
+TURN = 384
+CUTS = ((384, T), (0, 384, 896, T))
 SPLIT = (3,)
 Y_AT = 2
 
@@ -47,6 +52,7 @@ def tile_moe_res_mlp_gelu_kernel(tc, xT, xr, w1, w2, gate, offs, out):
         small = ctx.enter_context(tc.tile_pool(name="small", bufs=3))
         psum1 = ctx.enter_context(tc.psum_pool(name="psum1", bufs=2))
         psum2 = ctx.enter_context(tc.psum_pool(name="psum2", bufs=3))
+        psum3 = ctx.enter_context(tc.psum_pool(name="psum3", bufs=1))
 
         offsets = keep.tile([P, S // 16], U16, name="offsets")
 
@@ -60,7 +66,9 @@ def tile_moe_res_mlp_gelu_kernel(tc, xT, xr, w1, w2, gate, offs, out):
         for b in range(2):
             nc.vector.memset(sums[b][:], 0.0)
 
-        x_codes = [keep.tile([P, T], U32, name=f"x_codes{s}", align_bytes=64) for s in range(PASSES)]
+        x_codes = [keep.tile([P, WINDOW], U32, name=f"x_codes{s}", align_bytes=64) for s in range(PASSES)]
+        for s in range(PASSES - 1):
+            nc.vector.memset(x_codes[s][:, T:WINDOW], 0)
         g_codes = [{} for s in range(PASSES)]
         g_scales = {}
         identity = keep.tile([P, P], F32, name="identity")
@@ -84,8 +92,8 @@ def tile_moe_res_mlp_gelu_kernel(tc, xT, xr, w1, w2, gate, offs, out):
 
         items = [("x", s, chunk) for s in range(PASSES) for chunk in range(len(X_CHUNKS))]
         for e in range(E):
-            items += [("w1", e, s) for s in range(PASSES)]
-            items += [("w2", late, 0) for late in (e,)]
+            for s in range(PASSES):
+                items += [("w1", e, s)] + [("w2", late, 0) for late in range(E) if W2_AT[late] == (e, s)]
         last_w1 = [items.index(("w1", e, PASSES - 1)) for e in range(E)]
         loaded = {}
 
@@ -200,16 +208,21 @@ def tile_moe_res_mlp_gelu_kernel(tc, xT, xr, w1, w2, gate, offs, out):
                 )
 
         def gather(s, f):
-            late = f == 1 and s == PASSES - 1
-            jobs = [(g_codes[s], x_codes[s], U32, f"g_codes{s}_{f}", 0)]
+            if s < PASSES - 1:
+                whole = keep.tile([P, S], U32, name=f"g_codes{s}", align_bytes=64)
+                nc.vector.tensor_copy(whole[:], x_codes[s][:].indirect(offsets[:]))
+                g_codes[s][0], g_codes[s][1] = whole[:, 0:LIST_HALF], whole[:, LIST_HALF:S]
+                return
+            late = f == 1
+            jobs = [(g_codes[s], x_codes[s][:, 0:T], U32, f"g_codes{s}_{f}", 0)]
             if s == PASSES - 1:
-                jobs.append((g_scales, x_scales, U8, f"g_scales{f}", 4 * LIST_HALF))
+                jobs.append((g_scales, x_scales[:], U8, f"g_scales{f}", 4 * LIST_HALF))
             for target, window, dtype, name, at in jobs:
                 if late:
                     target[f] = shared.tile([P, LIST_HALF], dtype, name=name, align_bytes=64, offset=at)
                 else:
                     target[f] = keep.tile([P, LIST_HALF], dtype, name=name, align_bytes=64)
-                nc.vector.tensor_copy(target[f][:], window[:].indirect(offsets[:, 32 * f : 32 * (f + 1)]))
+                nc.vector.tensor_copy(target[f][:], window.indirect(offsets[:, 32 * f : 32 * (f + 1)]))
 
         def first_layer(e, s):
             if s == 0:
@@ -254,6 +267,8 @@ def tile_moe_res_mlp_gelu_kernel(tc, xT, xr, w1, w2, gate, offs, out):
             h_codes, h_scales = hidden[e]
             if (e, blocks) == (E - 2, (1,)):
                 bank = psum1.tile([P, 2, C], F32, name="a_bank")
+            elif TURN and e == E - 1:
+                bank = psum3.tile([P, 2, C], F32, name="late_bank")
             else:
                 bank = psum2.tile([P, 2, C], F32, name="y_bank")
             for b in blocks:
@@ -291,10 +306,31 @@ def tile_moe_res_mlp_gelu_kernel(tc, xT, xr, w1, w2, gate, offs, out):
             )
 
         def finish(b):
-            for c0, c1 in ((0, 640), (640, T)) if b == 0 else ((0, 512), (512, 1024), (1024, T)):
+            for c0, c1 in zip(CUTS[b], CUTS[b][1:]):
                 cols = slice(c0, c1)
                 nc.vector.tensor_tensor(residual[b][:, cols], sums[b][:, cols], residual[b][:, cols], ADD)
                 nc.sync.dma_start(out=out[P * b : P * (b + 1), cols], in_=residual[b][:, cols])
+
+        def turn(bank, src, first):
+            for at in range(0, TURN, P):
+                nc.tensor.matmul(
+                    bank[:, at : at + P],
+                    src[:, at : at + P],
+                    identity[:],
+                    start=(first and at == 0),
+                    stop=(not first and at == TURN - P),
+                    is_transpose=True,
+                )
+
+        def turn_back(turned):
+            by_token = keep.tile([P, TURN], F32, name="by_token")
+            nc.scalar.copy(out=by_token[:], in_=turned[:])
+            bank = psum1.tile([P, TURN], F32, name="a_bank")
+            for at in range(0, TURN, P):
+                nc.tensor.transpose(bank[:, at : at + P], by_token[:, at : at + P], identity[:])
+            done = keep.tile([P, TURN], F32, name="done")
+            nc.scalar.copy(out=done[:], in_=bank[:])
+            nc.scalar.dma_start(out=out[0:P, 0:TURN], in_=done[:])
 
         ahead = 12
         for item in items[:ahead]:
@@ -308,8 +344,6 @@ def tile_moe_res_mlp_gelu_kernel(tc, xT, xr, w1, w2, gate, offs, out):
                 quantize(item)
                 if item[0] == "x" and item[2] == len(X_CHUNKS) - 1:
                     gather(item[1], 0)
-                    if item[1] < PASSES - 1:
-                        gather(item[1], 1)
                 if item[0] == "w1":
                     first_layer(item[1], item[2])
                 if item == ("w2", 0, 0):
@@ -335,8 +369,22 @@ def tile_moe_res_mlp_gelu_kernel(tc, xT, xr, w1, w2, gate, offs, out):
         second_layer(E - 2, (1,))
         leave_bank(E - 2, (1,))
         put_back(E - 2, 1)
-        second_layer(E - 1, (0, 1))
-        leave_bank(E - 1, (0, 1))
-        for b in range(2):
-            put_back(E - 1, b)
-            finish(b)
+        if TURN:
+            turned = psum3.tile([P, TURN], F32, name="turned")
+            second_layer(E - 1, (0,))
+            leave_bank(E - 1, (0,))
+            second_layer(E - 1, (1,))
+            leave_bank(E - 1, (1,))
+            turn(turned, residual[0], True)
+            put_back(E - 1, 0)
+            turn(turned, sums[0], False)
+            finish(0)
+            turn_back(turned)
+            put_back(E - 1, 1)
+            finish(1)
+        else:
+            second_layer(E - 1, (0, 1))
+            leave_bank(E - 1, (0, 1))
+            for b in range(2):
+                put_back(E - 1, b)
+                finish(b)

@@ -22,23 +22,19 @@ ADD = mybir.AluOpType.add
 
 P = 128
 PASSES = K // 512
-LIST_HALF = 512
-WINDOW = 1408
+LAST_PASS = PASSES - 1
+LAST = E - 1
+LIST_HALF = S // 2
+WINDOW = T + 128
 X_CHUNKS = ((0, 512), (512, 512), (1024, 256))
-SLOT = 4 * H * 4
-SLOTS = 15
+X_TAIL_ON_VECTOR = (256, 128, 0)
+W2_ON_VECTOR = (1, 2)
+STORE_CUTS = ((0, 256, 768, T), (0, 512, 1024, T))
+CELL = 4 * H * 4
+CELLS = 15
 X_BYTES = 4 * T * 4
 FIRST_FREE = 8
-V_PASS = (1, 1, 1, 1)
-V_W2 = (1,2)
-V_X = ((1,2),(1,),(1,))
-H3 = 0
-W2_AT = ((0, 2), (1, 2), (2, 2), (3, 2))
-PARTS = 0
-TURN = 384
-CUTS = ((384, T), (0, 384, 896, T))
-SPLIT = (3,)
-Y_AT = 2
+AHEAD = 12
 
 
 def tile_moe_res_mlp_gelu_kernel(tc, xT, xr, w1, w2, gate, offs, out):
@@ -52,7 +48,6 @@ def tile_moe_res_mlp_gelu_kernel(tc, xT, xr, w1, w2, gate, offs, out):
         small = ctx.enter_context(tc.tile_pool(name="small", bufs=3))
         psum1 = ctx.enter_context(tc.psum_pool(name="psum1", bufs=2))
         psum2 = ctx.enter_context(tc.psum_pool(name="psum2", bufs=3))
-        psum3 = ctx.enter_context(tc.psum_pool(name="psum3", bufs=1))
 
         offsets = keep.tile([P, S // 16], U16, name="offsets")
 
@@ -67,10 +62,11 @@ def tile_moe_res_mlp_gelu_kernel(tc, xT, xr, w1, w2, gate, offs, out):
             nc.vector.memset(sums[b][:], 0.0)
 
         x_codes = [keep.tile([P, WINDOW], U32, name=f"x_codes{s}", align_bytes=64) for s in range(PASSES)]
-        for s in range(PASSES - 1):
+        for s in range(LAST_PASS):
             nc.vector.memset(x_codes[s][:, T:WINDOW], 0)
         g_codes = [{} for s in range(PASSES)]
         g_scales = {}
+
         identity = keep.tile([P, P], F32, name="identity")
         make_identity(nc, identity[:])
         gate_rows = keep.tile([P, 8], F32, name="gate_rows")
@@ -92,15 +88,12 @@ def tile_moe_res_mlp_gelu_kernel(tc, xT, xr, w1, w2, gate, offs, out):
 
         items = [("x", s, chunk) for s in range(PASSES) for chunk in range(len(X_CHUNKS))]
         for e in range(E):
-            for s in range(PASSES):
-                items += [("w1", e, s)] + [("w2", late, 0) for late in range(E) if W2_AT[late] == (e, s)]
-        last_w1 = [items.index(("w1", e, PASSES - 1)) for e in range(E)]
+            items += [("w1", e, s) for s in range(PASSES)] + [("w2", e, 0)]
         loaded = {}
-
         place = {}
 
-        def slot(item, shape):
-            place[item] = SLOT * ((FIRST_FREE + len(place)) % SLOTS)
+        def next_cell(item, shape):
+            place[item] = CELL * ((FIRST_FREE + len(place)) % CELLS)
             return over(item, 0, shape, F32, "rows")
 
         def over(item, at, shape, dtype, what):
@@ -117,20 +110,21 @@ def tile_moe_res_mlp_gelu_kernel(tc, xT, xr, w1, w2, gate, offs, out):
                 if item == ("x", 0, 0):
                     nc.sync.dma_start(offsets[:], offs)
             elif kind == "w1":
-                loaded[item] = slot(item, [P, 4, H])
+                loaded[item] = next_cell(item, [P, 4, H])
                 rows = w1[a, 512 * b : 512 * (b + 1), :]
                 nc.sync.dma_start(out=loaded[item][:], in_=rows.rearrange("(p j) w -> p j w", j=4))
             else:
-                w2_rows[a] = slot(item, [P, 4, N])
+                w2_rows[a] = next_cell(item, [P, 4, N])
                 nc.sync.dma_start(out=w2_rows[a][:], in_=w2[a].rearrange("(p j) w -> p j w", j=4))
-                if a == E - 1:
-                    for c in range(2):
-                        residual[c] = slot(("xr", c, 0), [P, T])
-                        nc.sync.dma_start(out=residual[c][:], in_=xr[P * c : P * (c + 1), :])
+                if a == LAST:
+                    for block in range(2):
+                        residual[block] = next_cell(("xr", block, 0), [P, T])
+                        nc.sync.dma_start(out=residual[block][:], in_=xr[P * block : P * (block + 1), :])
 
         grouped = {}
         weights = {}
         hidden = {}
+        h_words = {}
         banks = {}
         a_banks = {}
         results = {}
@@ -143,45 +137,44 @@ def tile_moe_res_mlp_gelu_kernel(tc, xT, xr, w1, w2, gate, offs, out):
             else:
                 nc.scalar.activation(out=dst, in_=src, func=COPY)
 
+        def half_of_w1(copy, wide, src, half):
+            dst = wide[:, 2 * H * half : 2 * H * (half + 1)].rearrange("p (t m j) -> p m j t", t=2, j=4)
+            copy(out=dst, in_=src[:, :, :, 2 * half : 2 * half + 2])
+
         def interleave(item):
             kind, a, b = item
             if kind == "w1":
                 src = loaded[item][:].rearrange("p j (m t) -> p m j t", t=4)
-                if (a, b) == (0, PASSES - 1):
-                    grouped[item] = shared.tile([P, 4 * H], BF16, name="first_last", align_bytes=64, offset=0)
+                if (a, b) == (0, LAST_PASS):
+                    wide = shared.tile([P, 4 * H], BF16, name="first_last", align_bytes=64, offset=0)
                 elif a > 0 and b == 1:
-                    grouped[item] = over(("w1", a, 0), SLOT // 2, [P, 4 * H], BF16, "wide")
+                    wide = over(("w1", a, 0), CELL // 2, [P, 4 * H], BF16, "wide")
                 else:
-                    grouped[item] = stage.tile([P, 4 * H], BF16, name="wide", align_bytes=64)
-                dst = grouped[item][:].rearrange("p (t m j) -> p m j t", t=4, j=4)
-                if a in SPLIT and b > 0:
-                    for half, copy in enumerate((nc.vector.tensor_copy, nc.scalar.copy)):
-                        part = grouped[item][:, 2 * H * half : 2 * H * (half + 1)]
-                        copy(
-                            out=part.rearrange("p (t m j) -> p m j t", t=2, j=4),
-                            in_=src[:, :, :, 2 * half : 2 * half + 2],
-                        )
-                elif b == V_PASS[a]:
-                    nc.vector.tensor_copy(out=dst, in_=src)
+                    wide = stage.tile([P, 4 * H], BF16, name="wide", align_bytes=64)
+                grouped[item] = wide
+                if a == LAST and b > 0:
+                    half_of_w1(nc.vector.tensor_copy, wide, src, 0)
+                    half_of_w1(nc.scalar.copy, wide, src, 1)
+                elif b == 1:
+                    nc.vector.tensor_copy(out=wide[:].rearrange("p (t m j) -> p m j t", t=4, j=4), in_=src)
                 else:
                     for half in range(2):
-                        part = grouped[item][:, 2 * H * half : 2 * H * (half + 1)]
-                        nc.scalar.copy(
-                            out=part.rearrange("p (t m j) -> p m j t", t=2, j=4),
-                            in_=src[:, :, :, 2 * half : 2 * half + 2],
-                        )
+                        half_of_w1(nc.scalar.copy, wide, src, half)
             elif kind == "x":
                 c0, width = X_CHUNKS[b]
-                engine = "V" if b in V_X[a] else "S"
                 wide = stage.tile([P, 4 * width], BF16, name="wide", align_bytes=64)
-                side_by_side(engine, wide[:], loaded[a][:, :, c0 : c0 + width])
+                cut = (0, width, X_TAIL_ON_VECTOR[a])[b]
+                if cut > 0:
+                    side_by_side("V", wide[:, 0 : 4 * cut], loaded[a][:, :, c0 : c0 + cut])
+                if cut < width:
+                    side_by_side("S", wide[:, 4 * cut :], loaded[a][:, :, c0 + cut : c0 + width])
                 grouped[item] = wide
             else:
-                if a > 0 and a not in V_W2:
-                    wide = over(("w1", a, Y_AT), SLOT // 2, [P, 4 * N], BF16, "wide")
+                if a == LAST:
+                    wide = over(("w1", a, LAST_PASS), CELL // 2, [P, 4 * N], BF16, "wide")
                 else:
                     wide = stage.tile([P, 4 * N], BF16, name="wide", align_bytes=64)
-                side_by_side("V" if a in V_W2 else "S", wide[:], w2_rows[a][:])
+                side_by_side("V" if a in W2_ON_VECTOR else "S", wide[:], w2_rows[a][:])
                 grouped[item] = wide
 
         def quantize(item):
@@ -207,22 +200,23 @@ def tile_moe_res_mlp_gelu_kernel(tc, xT, xr, w1, w2, gate, offs, out):
                     out=w2_codes[a][:].bitcast(FP8X4), scales=w2_scales[a][:], in_=grouped.pop(item)[:]
                 )
 
-        def gather(s, f):
-            if s < PASSES - 1:
-                whole = keep.tile([P, S], U32, name=f"g_codes{s}", align_bytes=64)
-                nc.vector.tensor_copy(whole[:], x_codes[s][:].indirect(offsets[:]))
-                g_codes[s][0], g_codes[s][1] = whole[:, 0:LIST_HALF], whole[:, LIST_HALF:S]
-                return
-            late = f == 1
-            jobs = [(g_codes[s], x_codes[s][:, 0:T], U32, f"g_codes{s}_{f}", 0)]
-            if s == PASSES - 1:
-                jobs.append((g_scales, x_scales[:], U8, f"g_scales{f}", 4 * LIST_HALF))
+        def gather_all_slots(s):
+            whole = keep.tile([P, S], U32, name=f"g_codes{s}", align_bytes=64)
+            nc.vector.tensor_copy(whole[:], x_codes[s][:].indirect(offsets[:]))
+            g_codes[s][0], g_codes[s][1] = whole[:, 0:LIST_HALF], whole[:, LIST_HALF:S]
+
+        def gather_last_pass(f):
+            jobs = (
+                (g_codes[LAST_PASS], x_codes[LAST_PASS][:, 0:T], U32, f"g_codes{LAST_PASS}_{f}", 0),
+                (g_scales, x_scales[:], U8, f"g_scales{f}", 4 * LIST_HALF),
+            )
+            entries = offsets[:, LIST_HALF // 16 * f : LIST_HALF // 16 * (f + 1)]
             for target, window, dtype, name, at in jobs:
-                if late:
+                if f == 1:
                     target[f] = shared.tile([P, LIST_HALF], dtype, name=name, align_bytes=64, offset=at)
                 else:
                     target[f] = keep.tile([P, LIST_HALF], dtype, name=name, align_bytes=64)
-                nc.vector.tensor_copy(target[f][:], window.indirect(offsets[:, 32 * f : 32 * (f + 1)]))
+                nc.vector.tensor_copy(target[f][:], window.indirect(entries))
 
         def first_layer(e, s):
             if s == 0:
@@ -239,14 +233,12 @@ def tile_moe_res_mlp_gelu_kernel(tc, xT, xr, w1, w2, gate, offs, out):
                         rhs=g_codes[s][f][:, at : at + P].bitcast(FP8X4),
                         rhs_scale=g_scales[f][4 * s : P, at : at + P],
                         start=(s == 0 and t == 0),
-                        stop=(s == PASSES - 1 and t == 3),
+                        stop=(s == LAST_PASS and t == 3),
                     )
 
         def activate(e):
-            if e < E - 1:
+            if e < LAST:
                 hidden[e] = over(("w1", e + 1, 0), 0, [P, 4 * C], BF16, "h")[:]
-            elif H3:
-                hidden[e] = over(("w2", e, 0), 0, [P, 4 * C], BF16, "h")[:]
             else:
                 hidden[e] = small.tile([P, 4 * C], BF16, name="h", align_bytes=64)[:]
             for part in range(2):
@@ -261,14 +253,12 @@ def tile_moe_res_mlp_gelu_kernel(tc, xT, xr, w1, w2, gate, offs, out):
             h_codes = small.tile([P, C], U32, name="h_codes", align_bytes=64)
             h_scales = small.tile([P, C], U8, name="h_scales", align_bytes=64)
             nc.vector.quantize_mx(out=h_codes[:].bitcast(FP8X4), scales=h_scales[:], in_=hidden[e])
-            hidden[e] = (h_codes, h_scales)
+            h_words[e] = (h_codes, h_scales)
 
         def second_layer(e, blocks):
-            h_codes, h_scales = hidden[e]
-            if (e, blocks) == (E - 2, (1,)):
+            h_codes, h_scales = h_words[e]
+            if (e, blocks) == (LAST - 1, (1,)):
                 bank = psum1.tile([P, 2, C], F32, name="a_bank")
-            elif TURN and e == E - 1:
-                bank = psum3.tile([P, 2, C], F32, name="late_bank")
             else:
                 bank = psum2.tile([P, 2, C], F32, name="y_bank")
             for b in blocks:
@@ -285,106 +275,75 @@ def tile_moe_res_mlp_gelu_kernel(tc, xT, xr, w1, w2, gate, offs, out):
                 banks[e, b] = bank
 
         def leave_bank(e, blocks):
-            if e < E - 2 and len(blocks) == 2:
-                both = over(("w1", e + 1, Y_AT), 0, [P, 2, C], F32, "y")
+            if e < LAST - 1:
+                both = over(("w1", e + 1, LAST_PASS), 0, [P, 2, C], F32, "y")
                 nc.scalar.copy(out=both[:], in_=banks[e, 0][:])
                 results[e, 0], results[e, 1] = both[:, 0, :], both[:, 1, :]
                 return
             for b in blocks:
-                if (e, b) == (E - 2, 0):
-                    results[e, b] = over(("w1", e + 1, Y_AT), 0, [P, C], F32, "y")[:]
+                if (e, b) == (LAST - 1, 0):
+                    results[e, b] = over(("w1", LAST, LAST_PASS), CELL // 4, [P, C], F32, "y")[:]
                 else:
                     results[e, b] = small.tile([P, C], F32, name=f"y{b}")[:]
                 nc.scalar.copy(out=results[e, b], in_=banks[e, b][:, b, :])
 
         def put_back(e, b):
             nc.vector.tensor_tensor(
-                sums[b][:].indirect(offsets[:, 16 * e : 16 * (e + 1)]),
+                sums[b][:].indirect(offsets[:, C // 16 * e : C // 16 * (e + 1)]),
                 results[e, b],
                 gates[:, C * e : C * (e + 1)],
                 MULT,
             )
 
         def finish(b):
-            for c0, c1 in zip(CUTS[b], CUTS[b][1:]):
+            for c0, c1 in zip(STORE_CUTS[b], STORE_CUTS[b][1:]):
                 cols = slice(c0, c1)
                 nc.vector.tensor_tensor(residual[b][:, cols], sums[b][:, cols], residual[b][:, cols], ADD)
                 nc.sync.dma_start(out=out[P * b : P * (b + 1), cols], in_=residual[b][:, cols])
 
-        def turn(bank, src, first):
-            for at in range(0, TURN, P):
-                nc.tensor.matmul(
-                    bank[:, at : at + P],
-                    src[:, at : at + P],
-                    identity[:],
-                    start=(first and at == 0),
-                    stop=(not first and at == TURN - P),
-                    is_transpose=True,
-                )
-
-        def turn_back(turned):
-            by_token = keep.tile([P, TURN], F32, name="by_token")
-            nc.scalar.copy(out=by_token[:], in_=turned[:])
-            bank = psum1.tile([P, TURN], F32, name="a_bank")
-            for at in range(0, TURN, P):
-                nc.tensor.transpose(bank[:, at : at + P], by_token[:, at : at + P], identity[:])
-            done = keep.tile([P, TURN], F32, name="done")
-            nc.scalar.copy(out=done[:], in_=bank[:])
-            nc.scalar.dma_start(out=out[0:P, 0:TURN], in_=done[:])
-
-        ahead = 12
-        for item in items[:ahead]:
+        for item in items[:AHEAD]:
             load(item)
         for step in range(len(items) - 1):
             interleave(items[step])
-            if step + ahead < len(items):
-                load(items[step + ahead])
+            if step + AHEAD < len(items):
+                load(items[step + AHEAD])
             if step >= 1:
-                item = items[step - 1]
-                quantize(item)
-                if item[0] == "x" and item[2] == len(X_CHUNKS) - 1:
-                    gather(item[1], 0)
-                if item[0] == "w1":
-                    first_layer(item[1], item[2])
-                if item == ("w2", 0, 0):
-                    gather(PASSES - 1, 1)
-            for e in range(E - 1):
+                kind, a, b = items[step - 1]
+                quantize(items[step - 1])
+                if kind == "x" and b == len(X_CHUNKS) - 1:
+                    if a < LAST_PASS:
+                        gather_all_slots(a)
+                    else:
+                        gather_last_pass(0)
+                if kind == "w1":
+                    first_layer(a, b)
+                if (kind, a) == ("w2", 0):
+                    gather_last_pass(1)
+            for e in range(LAST):
+                blocks = (0, 1) if e < LAST - 1 else (0,)
                 if items[step] == ("w1", e + 1, 0):
                     activate(e)
                 if items[step] == ("w1", e + 1, 1):
                     quantize_hidden(e)
-                    second_layer(e, (0, 1) if e < E - 2 else (0,))
-                if items[step] == ("w1", e + 1, 2):
-                    leave_bank(e, (0, 1) if e < E - 2 else (0,))
+                    second_layer(e, blocks)
+                if items[step] == ("w1", e + 1, LAST_PASS):
+                    leave_bank(e, blocks)
                 if items[step] == ("w1", e + 2, 0):
                     put_back(e, 0)
                     put_back(e, 1)
-        quantize(("w1", E - 1, PASSES - 1))
-        first_layer(E - 1, PASSES - 1)
-        put_back(E - 2, 0)
-        interleave(("w2", E - 1, 0))
-        quantize(("w2", E - 1, 0))
-        activate(E - 1)
-        quantize_hidden(E - 1)
-        second_layer(E - 2, (1,))
-        leave_bank(E - 2, (1,))
-        put_back(E - 2, 1)
-        if TURN:
-            turned = psum3.tile([P, TURN], F32, name="turned")
-            second_layer(E - 1, (0,))
-            leave_bank(E - 1, (0,))
-            second_layer(E - 1, (1,))
-            leave_bank(E - 1, (1,))
-            turn(turned, residual[0], True)
-            put_back(E - 1, 0)
-            turn(turned, sums[0], False)
-            finish(0)
-            turn_back(turned)
-            put_back(E - 1, 1)
-            finish(1)
-        else:
-            second_layer(E - 1, (0, 1))
-            leave_bank(E - 1, (0, 1))
-            for b in range(2):
-                put_back(E - 1, b)
-                finish(b)
+
+        quantize(("w1", LAST, LAST_PASS))
+        first_layer(LAST, LAST_PASS)
+        put_back(LAST - 1, 0)
+        interleave(("w2", LAST, 0))
+        quantize(("w2", LAST, 0))
+        activate(LAST)
+        quantize_hidden(LAST)
+        second_layer(LAST - 1, (1,))
+        leave_bank(LAST - 1, (1,))
+        put_back(LAST - 1, 1)
+        second_layer(LAST, (0, 1))
+        leave_bank(LAST, (0, 1))
+        for b in range(2):
+            put_back(LAST, b)
+            finish(b)

@@ -29,7 +29,8 @@ WINDOW = T + 128
 X_CHUNKS = ((0, 512), (512, 512), (1024, 256))
 X_TAIL_ON_VECTOR = (256, 128, 0)
 W2_ON_VECTOR = (1, 2)
-STORE_CUTS = ((0, 256, 768, T), (0, 512, 1024, T))
+STORE_CUTS = ((0, 512, 1024, T), (0, 512, 1024, T))
+END_CUTS = (512, 704, 864, S)
 CELL = 4 * H * 4
 CELLS = 15
 X_BYTES = 4 * T * 4
@@ -82,6 +83,7 @@ def tile_moe_res_mlp_gelu_kernel(tc, xT, xr, w1, w2, gate, offs, out):
                 in_=spread[:].rearrange("p c n -> p n c"),
             )
         residual = {}
+        y_end = keep.tile([P, 2 * C], F32, name="y_end")
         w2_rows = {}
         w2_codes = [keep.tile([P, N], U32, name=f"w2_codes{e}", align_bytes=64) for e in range(E)]
         w2_scales = [keep.tile([P, N], U8, name=f"w2_scales{e}", align_bytes=64) for e in range(E)]
@@ -191,10 +193,16 @@ def tile_moe_res_mlp_gelu_kernel(tc, xT, xr, w1, w2, gate, offs, out):
                     scales = w_pool.tile([P, PASSES * H], U8, name="w1_scales", align_bytes=64)
                     weights[a] = (codes, scales)
                 codes, scales = weights[a]
-                cols = slice(H * b, H * (b + 1))
-                nc.vector.quantize_mx(
-                    out=codes[:, cols].bitcast(FP8X4), scales=scales[:, cols], in_=grouped.pop(item)[:]
-                )
+                wide = grouped.pop(item)
+                pieces = 2 if (a, b) == (LAST, LAST_PASS) else 1
+                width = H // pieces
+                for piece in range(pieces):
+                    cols = slice(H * b + width * piece, H * b + width * (piece + 1))
+                    nc.vector.quantize_mx(
+                        out=codes[:, cols].bitcast(FP8X4),
+                        scales=scales[:, cols],
+                        in_=wide[:, 4 * width * piece : 4 * width * (piece + 1)],
+                    )
             else:
                 nc.vector.quantize_mx(
                     out=w2_codes[a][:].bitcast(FP8X4), scales=w2_scales[a][:], in_=grouped.pop(item)[:]
@@ -222,9 +230,9 @@ def tile_moe_res_mlp_gelu_kernel(tc, xT, xr, w1, w2, gate, offs, out):
             if s == 0:
                 a_banks[e] = [psum1.tile([P, 4, P], F32, name="a_bank") for part in range(2)]
             codes, scales = weights[e]
-            for part in range(2):
+            for half, part in ((0, 0), (0, 1), (1, 0), (1, 1)):
                 f, at = divmod(C * e + P * part, LIST_HALF)
-                for t in range(4):
+                for t in (2 * half, 2 * half + 1):
                     rows = slice(H * s + P * t, H * s + P * (t + 1))
                     nc.tensor.matmul_mx(
                         out=a_banks[e][part][:, t, :],
@@ -283,6 +291,8 @@ def tile_moe_res_mlp_gelu_kernel(tc, xT, xr, w1, w2, gate, offs, out):
             for b in blocks:
                 if (e, b) == (LAST - 1, 0):
                     results[e, b] = over(("w1", LAST, LAST_PASS), CELL // 4, [P, C], F32, "y")[:]
+                elif b == 1:
+                    results[e, b] = y_end[:, C * (e - 2) : C * (e - 1)]
                 else:
                     results[e, b] = small.tile([P, C], F32, name=f"y{b}")[:]
                 nc.scalar.copy(out=results[e, b], in_=banks[e, b][:, b, :])
@@ -295,9 +305,18 @@ def tile_moe_res_mlp_gelu_kernel(tc, xT, xr, w1, w2, gate, offs, out):
                 MULT,
             )
 
-        def finish(b):
-            for c0, c1 in zip(STORE_CUTS[b], STORE_CUTS[b][1:]):
-                cols = slice(c0, c1)
+        def put_back_end(piece):
+            s0, s1 = END_CUTS[piece], END_CUTS[piece + 1]
+            nc.vector.tensor_tensor(
+                sums[1][:].indirect(offsets[:, s0 // 16 : s1 // 16]),
+                y_end[:, s0 - 2 * C : s1 - 2 * C],
+                gates[:, s0:s1],
+                MULT,
+            )
+
+        def finish(b, pieces):
+            for piece in pieces:
+                cols = slice(STORE_CUTS[b][piece], STORE_CUTS[b][piece + 1])
                 nc.vector.tensor_tensor(residual[b][:, cols], sums[b][:, cols], residual[b][:, cols], ADD)
                 nc.sync.dma_start(out=out[P * b : P * (b + 1), cols], in_=residual[b][:, cols])
 
@@ -341,9 +360,12 @@ def tile_moe_res_mlp_gelu_kernel(tc, xT, xr, w1, w2, gate, offs, out):
         quantize_hidden(LAST)
         second_layer(LAST - 1, (1,))
         leave_bank(LAST - 1, (1,))
-        put_back(LAST - 1, 1)
+        put_back_end(0)
         second_layer(LAST, (0, 1))
         leave_bank(LAST, (0, 1))
-        for b in range(2):
-            put_back(LAST, b)
-            finish(b)
+        put_back(LAST, 0)
+        put_back_end(1)
+        finish(0, (0, 1))
+        put_back_end(2)
+        finish(0, (2,))
+        finish(1, (0, 1, 2))

@@ -27,7 +27,7 @@ LAST = E - 1
 LIST_HALF = S // 2
 WINDOW = T + 128
 X_CHUNKS = ((0, 512), (512, 512), (1024, 256))
-X_TAIL_ON_VECTOR = (256, 128, 0)
+X_TAIL_ON_VECTOR = (256, 128, 128)
 W2_ON_VECTOR = (1, 2)
 STORE_CUTS = ((0, 512, 1024, T), (0, 512, 1024, T))
 END_CUTS = (512, 704, 864, S)
@@ -154,7 +154,7 @@ def tile_moe_res_mlp_gelu_kernel(tc, xT, xr, w1, w2, gate, offs, out):
                 else:
                     wide = stage.tile([P, 4 * H], BF16, name="wide", align_bytes=64)
                 grouped[item] = wide
-                if a == LAST and b > 0:
+                if (a == LAST and b > 0) or (a, b) == (0, 1):
                     half_of_w1(nc.vector.tensor_copy, wide, src, 0)
                     half_of_w1(nc.scalar.copy, wide, src, 1)
                 elif b == 1:

from contextlib import ExitStack

import concourse.mybir as mybir
from concourse.masks import make_identity

K, T, E, C, H, N = 1536, 1280, 4, 256, 512, 256
S = E * C

FLOPS = 2 * S * K * H + 2 * S * H * N
BYTES = 4 * (K * T + 2 * N * T + E * K * H + E * H * N + S) + 2 * 128 * (S // 16)

F32 = mybir.dt.float32
BF16 = mybir.dt.bfloat16
U32 = mybir.dt.uint32
U16 = mybir.dt.uint16
U8 = mybir.dt.uint8
FP8X4 = mybir.dt.float8_e4m3fn_x4
COPY = mybir.ActivationFunctionType.Copy
GELU = mybir.ActivationFunctionType.Gelu_apprx_tanh
MULT = mybir.AluOpType.mult
ADD = mybir.AluOpType.add

P = 128
PASSES = K // 512
LAST_PASS = PASSES - 1
LAST = E - 1
LIST_HALF = S // 2
WINDOW = T + 128
X_CHUNKS = ((0, 512), (512, 512), (1024, 256))
X_TAIL_ON_VECTOR = (256, 128, 128)
W2_ON_VECTOR = (1, 2)
STORE_CUTS = ((0, 512, 1024, T), (0, 512, 1024, T))
END_CUTS = (512, 704, 864, S)
CELL = 4 * H * 4
CELLS = 15
X_BYTES = 4 * T * 4
FIRST_FREE = 8
AHEAD = 12


def tile_moe_res_mlp_gelu_kernel(tc, xT, xr, w1, w2, gate, offs, out):
    nc = tc.nc
    with ExitStack() as ctx:
        keep = ctx.enter_context(tc.tile_pool(name="keep", bufs=1))
        rows_pool = ctx.enter_context(tc.tile_pool(name="rows_pool", bufs=1))
        stage = ctx.enter_context(tc.tile_pool(name="stage", bufs=6))
        shared = ctx.enter_context(tc.tile_pool(name="shared", bufs=1))
        w_pool = ctx.enter_context(tc.tile_pool(name="w_pool", bufs=2))
        small = ctx.enter_context(tc.tile_pool(name="small", bufs=3))
        psum1 = ctx.enter_context(tc.psum_pool(name="psum1", bufs=2))
        psum2 = ctx.enter_context(tc.psum_pool(name="psum2", bufs=3))

        offsets = keep.tile([P, S // 16], U16, name="offsets")

        warm = keep.tile([P, 2], F32, name="warm")
        nc.vector.memset(warm[:], 0.0)
        nc.scalar.activation(out=warm[:, 1:2], in_=warm[:, 0:1], func=GELU)

        x_scales = keep.tile([P, T], U8, name="x_scales", align_bytes=64)
        nc.vector.memset(x_scales[:].bitcast(U32), 0)
        sums = [keep.tile([P, T], F32, name=f"sums{b}") for b in range(2)]
        for b in range(2):
            nc.vector.memset(sums[b][:], 0.0)

        x_codes = [keep.tile([P, WINDOW], U32, name=f"x_codes{s}", align_bytes=64) for s in range(PASSES)]
        for s in range(LAST_PASS):
            nc.vector.memset(x_codes[s][:, T:WINDOW], 0)
        g_codes = [{} for s in range(PASSES)]
        g_scales = {}

        identity = keep.tile([P, P], F32, name="identity")
        make_identity(nc, identity[:])
        gate_rows = keep.tile([P, 8], F32, name="gate_rows")
        nc.scalar.dma_start(out=gate_rows[:], in_=gate[0:1, :].rearrange("o (p c) -> (o p) c", c=8))
        gates = keep.tile([P, S], F32, name="gates")
        for half in range(2):
            spread = psum1.tile([P, 4, P], F32, name="a_bank")
            for c in range(4):
                column = gate_rows[:, 4 * half + c : 4 * half + c + 1]
                nc.tensor.transpose(spread[:, c, :], column.to_broadcast([P, P]), identity[:])
            nc.scalar.copy(
                out=gates[:].rearrange("p (n c) -> p n c", c=8)[:, :, 4 * half : 4 * half + 4],
                in_=spread[:].rearrange("p c n -> p n c"),
            )
        residual = {}
        y_end = keep.tile([P, 2 * C], F32, name="y_end")
        w2_rows = {}
        w2_codes = [keep.tile([P, N], U32, name=f"w2_codes{e}", align_bytes=64) for e in range(E)]
        w2_scales = [keep.tile([P, N], U8, name=f"w2_scales{e}", align_bytes=64) for e in range(E)]

        items = [("x", s, chunk) for s in range(PASSES) for chunk in range(len(X_CHUNKS))]
        for e in range(E):
            items += [("w1", e, s) for s in range(PASSES)] + [("w2", e, 0)]
        loaded = {}
        place = {}

        def next_cell(item, shape):
            place[item] = CELL * ((FIRST_FREE + len(place)) % CELLS)
            return over(item, 0, shape, F32, "rows")

        def over(item, at, shape, dtype, what):
            name = what + "".join(f"_{part}" for part in item)
            return rows_pool.tile(shape, dtype, name=name, align_bytes=64, offset=place[item] + at)

        def load(item):
            kind, a, b = item
            if kind == "x":
                if b == 0:
                    loaded[a] = rows_pool.tile([P, 4, T], F32, name=f"x_rows{a}", align_bytes=64, offset=X_BYTES * a)
                    rows = xT[512 * a : 512 * (a + 1), :]
                    nc.sync.dma_start(out=loaded[a][:], in_=rows.rearrange("(p j) w -> p j w", j=4))
                if item == ("x", 0, 0):
                    nc.sync.dma_start(offsets[:], offs)
            elif kind == "w1":
                loaded[item] = next_cell(item, [P, 4, H])
                rows = w1[a, 512 * b : 512 * (b + 1), :]
                nc.sync.dma_start(out=loaded[item][:], in_=rows.rearrange("(p j) w -> p j w", j=4))
            else:
                w2_rows[a] = next_cell(item, [P, 4, N])
                nc.sync.dma_start(out=w2_rows[a][:], in_=w2[a].rearrange("(p j) w -> p j w", j=4))
                if a == LAST:
                    for block in range(2):
                        residual[block] = next_cell(("xr", block, 0), [P, T])
                        nc.sync.dma_start(out=residual[block][:], in_=xr[P * block : P * (block + 1), :])

        grouped = {}
        weights = {}
        hidden = {}
        h_words = {}
        banks = {}
        a_banks = {}
        results = {}

        def side_by_side(engine, dst, src):
            dst = dst.rearrange("p (c i j) -> p c j i", i=2, j=4)
            src = src.rearrange("p j (c i) -> p c j i", i=2)
            if engine == "V":
                nc.vector.tensor_copy(out=dst, in_=src)
            else:
                nc.scalar.activation(out=dst, in_=src, func=COPY)

        def half_of_w1(copy, wide, src, half):
            dst = wide[:, 2 * H * half : 2 * H * (half + 1)].rearrange("p (t m j) -> p m j t", t=2, j=4)
            copy(out=dst, in_=src[:, :, :, 2 * half : 2 * half + 2])

        def interleave(item):
            kind, a, b = item
            if kind == "w1":
                src = loaded[item][:].rearrange("p j (m t) -> p m j t", t=4)
                if (a, b) == (0, LAST_PASS):
                    wide = shared.tile([P, 4 * H], BF16, name="first_last", align_bytes=64, offset=0)
                elif a > 0 and b == 1:
                    wide = over(("w1", a, 0), CELL // 2, [P, 4 * H], BF16, "wide")
                else:
                    wide = stage.tile([P, 4 * H], BF16, name="wide", align_bytes=64)
                grouped[item] = wide
                if (a == LAST and b > 0) or (a, b) == (0, 1):
                    half_of_w1(nc.vector.tensor_copy, wide, src, 0)
                    half_of_w1(nc.scalar.copy, wide, src, 1)
                elif b == 1:
                    nc.vector.tensor_copy(out=wide[:].rearrange("p (t m j) -> p m j t", t=4, j=4), in_=src)
                else:
                    for half in range(2):
                        half_of_w1(nc.scalar.copy, wide, src, half)
            elif kind == "x":
                c0, width = X_CHUNKS[b]
                wide = stage.tile([P, 4 * width], BF16, name="wide", align_bytes=64)
                cut = (0, width, X_TAIL_ON_VECTOR[a])[b]
                if cut > 0:
                    side_by_side("V", wide[:, 0 : 4 * cut], loaded[a][:, :, c0 : c0 + cut])
                if cut < width:
                    side_by_side("S", wide[:, 4 * cut :], loaded[a][:, :, c0 + cut : c0 + width])
                grouped[item] = wide
            else:
                if a == LAST:
                    wide = over(("w1", a, LAST_PASS), CELL // 2, [P, 4 * N], BF16, "wide")
                else:
                    wide = stage.tile([P, 4 * N], BF16, name="wide", align_bytes=64)
                side_by_side("V" if a in W2_ON_VECTOR else "S", wide[:], w2_rows[a][:])
                grouped[item] = wide

        def quantize(item):
            kind, a, b = item
            if kind == "x":
                c0, width = X_CHUNKS[b]
                cols = slice(c0, c0 + width)
                nc.vector.quantize_mx(
                    out=x_codes[a][:, cols].bitcast(FP8X4), scales=x_scales[4 * a : P, cols], in_=grouped.pop(item)[:]
                )
            elif kind == "w1":
                if b == 0:
                    codes = w_pool.tile([P, PASSES * H], U32, name="w1_codes", align_bytes=64)
                    scales = w_pool.tile([P, PASSES * H], U8, name="w1_scales", align_bytes=64)
                    weights[a] = (codes, scales)
                codes, scales = weights[a]
                wide = grouped.pop(item)
                pieces = 2 if (a, b) == (LAST, LAST_PASS) else 1
                width = H // pieces
                for piece in range(pieces):
                    cols = slice(H * b + width * piece, H * b + width * (piece + 1))
                    nc.vector.quantize_mx(
                        out=codes[:, cols].bitcast(FP8X4),
                        scales=scales[:, cols],
                        in_=wide[:, 4 * width * piece : 4 * width * (piece + 1)],
                    )
            else:
                nc.vector.quantize_mx(
                    out=w2_codes[a][:].bitcast(FP8X4), scales=w2_scales[a][:], in_=grouped.pop(item)[:]
                )

        def gather_all_slots(s):
            whole = keep.tile([P, S], U32, name=f"g_codes{s}", align_bytes=64)
            nc.vector.tensor_copy(whole[:], x_codes[s][:].indirect(offsets[:]))
            g_codes[s][0], g_codes[s][1] = whole[:, 0:LIST_HALF], whole[:, LIST_HALF:S]

        def gather_last_pass(f):
            jobs = (
                (g_codes[LAST_PASS], x_codes[LAST_PASS][:, 0:T], U32, f"g_codes{LAST_PASS}_{f}", 0),
                (g_scales, x_scales[:], U8, f"g_scales{f}", 4 * LIST_HALF),
            )
            entries = offsets[:, LIST_HALF // 16 * f : LIST_HALF // 16 * (f + 1)]
            for target, window, dtype, name, at in jobs:
                if f == 1:
                    target[f] = shared.tile([P, LIST_HALF], dtype, name=name, align_bytes=64, offset=at)
                else:
                    target[f] = keep.tile([P, LIST_HALF], dtype, name=name, align_bytes=64)
                nc.vector.tensor_copy(target[f][:], window.indirect(entries))

        def first_layer(e, s):
            if s == 0:
                a_banks[e] = [psum1.tile([P, 4, P], F32, name="a_bank") for part in range(2)]
            codes, scales = weights[e]
            for half, part in ((0, 0), (0, 1), (1, 0), (1, 1)):
                f, at = divmod(C * e + P * part, LIST_HALF)
                for t in (2 * half, 2 * half + 1):
                    rows = slice(H * s + P * t, H * s + P * (t + 1))
                    nc.tensor.matmul_mx(
                        out=a_banks[e][part][:, t, :],
                        lhsT=codes[:, rows].bitcast(FP8X4),
                        lhsT_scale=scales[:, rows],
                        rhs=g_codes[s][f][:, at : at + P].bitcast(FP8X4),
                        rhs_scale=g_scales[f][4 * s : P, at : at + P],
                        start=(s == 0 and t == 0),
                        stop=(s == LAST_PASS and t == 3),
                    )

        def activate(e):
            if e < LAST:
                hidden[e] = over(("w1", e + 1, 0), 0, [P, 4 * C], BF16, "h")[:]
            else:
                hidden[e] = small.tile([P, 4 * C], BF16, name="h", align_bytes=64)[:]
            for part in range(2):
                h = hidden[e][:, 4 * P * part : 4 * P * (part + 1)]
                nc.scalar.activation(
                    out=h.rearrange("p (n t) -> p n t", t=4),
                    in_=a_banks[e][part][:].rearrange("p t n -> p n t"),
                    func=GELU,
                )

        def quantize_hidden(e):
            h_codes = small.tile([P, C], U32, name="h_codes", align_bytes=64)
            h_scales = small.tile([P, C], U8, name="h_scales", align_bytes=64)
            nc.vector.quantize_mx(out=h_codes[:].bitcast(FP8X4), scales=h_scales[:], in_=hidden[e])
            h_words[e] = (h_codes, h_scales)

        def second_layer(e, blocks):
            h_codes, h_scales = h_words[e]
            if (e, blocks) == (LAST - 1, (1,)):
                bank = psum1.tile([P, 2, C], F32, name="a_bank")
            else:
                bank = psum2.tile([P, 2, C], F32, name="y_bank")
            for b in blocks:
                rows = slice(P * b, P * (b + 1))
                nc.tensor.matmul_mx(
                    out=bank[:, b, :],
                    lhsT=w2_codes[e][:, rows].bitcast(FP8X4),
                    lhsT_scale=w2_scales[e][:, rows],
                    rhs=h_codes[:].bitcast(FP8X4),
                    rhs_scale=h_scales[:],
                    start=True,
                    stop=True,
                )
                banks[e, b] = bank

        def leave_bank(e, blocks):
            if e < LAST - 1:
                both = over(("w1", e + 1, LAST_PASS), 0, [P, 2, C], F32, "y")
                nc.scalar.copy(out=both[:], in_=banks[e, 0][:])
                results[e, 0], results[e, 1] = both[:, 0, :], both[:, 1, :]
                return
            for b in blocks:
                if (e, b) == (LAST - 1, 0):
                    results[e, b] = over(("w1", LAST, LAST_PASS), CELL // 4, [P, C], F32, "y")[:]
                elif b == 1:
                    results[e, b] = y_end[:, C * (e - 2) : C * (e - 1)]
                else:
                    results[e, b] = small.tile([P, C], F32, name=f"y{b}")[:]
                nc.scalar.copy(out=results[e, b], in_=banks[e, b][:, b, :])

        def put_back(e, b):
            nc.vector.tensor_tensor(
                sums[b][:].indirect(offsets[:, C // 16 * e : C // 16 * (e + 1)]),
                results[e, b],
                gates[:, C * e : C * (e + 1)],
                MULT,
            )

        def put_back_end(piece):
            s0, s1 = END_CUTS[piece], END_CUTS[piece + 1]
            nc.vector.tensor_tensor(
                sums[1][:].indirect(offsets[:, s0 // 16 : s1 // 16]),
                y_end[:, s0 - 2 * C : s1 - 2 * C],
                gates[:, s0:s1],
                MULT,
            )

        def finish(b, pieces):
            for piece in pieces:
                cols = slice(STORE_CUTS[b][piece], STORE_CUTS[b][piece + 1])
                nc.vector.tensor_tensor(residual[b][:, cols], sums[b][:, cols], residual[b][:, cols], ADD)
                nc.sync.dma_start(out=out[P * b : P * (b + 1), cols], in_=residual[b][:, cols])

        for item in items[:AHEAD]:
            load(item)
        for step in range(len(items) - 1):
            interleave(items[step])
            if step + AHEAD < len(items):
                load(items[step + AHEAD])
            if step >= 1:
                kind, a, b = items[step - 1]
                quantize(items[step - 1])
                if kind == "x" and b == len(X_CHUNKS) - 1:
                    if a < LAST_PASS:
                        gather_all_slots(a)
                    else:
                        gather_last_pass(0)
                if kind == "w1":
                    first_layer(a, b)
                if (kind, a) == ("w2", 0):
                    gather_last_pass(1)
            for e in range(LAST):
                blocks = (0, 1) if e < LAST - 1 else (0,)
                if items[step] == ("w1", e + 1, 0):
                    activate(e)
                if items[step] == ("w1", e + 1, 1):
                    quantize_hidden(e)
                    second_layer(e, blocks)
                if items[step] == ("w1", e + 1, LAST_PASS):
                    leave_bank(e, blocks)
                if items[step] == ("w1", e + 2, 0):
                    put_back(e, 0)
                    put_back(e, 1)

        quantize(("w1", LAST, LAST_PASS))
        first_layer(LAST, LAST_PASS)
        put_back(LAST - 1, 0)
        interleave(("w2", LAST, 0))
        quantize(("w2", LAST, 0))
        activate(LAST)
        quantize_hidden(LAST)
        second_layer(LAST - 1, (1,))
        leave_bank(LAST - 1, (1,))
        put_back_end(0)
        second_layer(LAST, (0, 1))
        leave_bank(LAST, (0, 1))
        put_back(LAST, 0)
        put_back_end(1)
        finish(0, (0, 1))
        put_back_end(2)
        finish(0, (2,))
        finish(1, (0, 1, 2))
